import numpy as np
import ml_dtypes


def mxq(x, axis, fmt="e4m3"):
    dtype, down = {"e4m3": (ml_dtypes.float8_e4m3fn, 7), "e5m2": (ml_dtypes.float8_e5m2, 14)}[fmt]
    v = np.moveaxis(np.asarray(x, np.float32).astype(ml_dtypes.bfloat16).astype(np.float64), axis, -1)
    blocks = v.reshape(v.shape[:-1] + (-1, 32))
    amax = np.abs(blocks).max(-1, keepdims=True)
    byte = np.maximum(np.where(amax > 0, np.frexp(amax)[1] - 1 + 127, 0) - down, 1)
    scale = np.exp2(byte - 127.0)
    codes = (blocks / scale).astype(np.float32).astype(dtype).astype(np.float64)
    return np.moveaxis((codes * scale).reshape(v.shape), -1, axis)


WIDE = False


def mx_kscale(k):
    if not WIDE:
        return np.ones(k)
    levels = np.array([10, -10, 5, -5, 0])
    if k % 512:
        return np.exp2(np.random.permutation(np.resize(levels, k // 32))).repeat(32)
    a = np.empty((k // 512, 16))
    for p in range(k // 512):
        a[p, :8] = np.random.permutation(np.resize(levels, 8))
        for g in range(8):
            far = levels[np.abs(levels - a[p, g]) >= 10]
            a[p, g + 8] = far[np.random.randint(len(far))]
    return np.exp2(a.ravel()).repeat(32)


def f64(x):
    return np.asarray(x).astype(np.float64)


def striped(idx):
    return np.tile(idx.reshape(-1, 16).T, (8, 1)).astype(np.uint16)


def unstriped(offs):
    return offs[:16].T.reshape(-1).astype(np.int64)


E2M1 = np.array([0.0, 0.5, 1.0, 1.5, 2.0, 3.0, 4.0, 6.0, -0.0, -0.5, -1.0, -1.5, -2.0, -3.0, -4.0, -6.0])


def pack_weight(w, fmt):
    k, n = w.shape
    w = f64(np.asarray(w, np.float32).astype(ml_dtypes.bfloat16)).reshape(k // 32, 32, n)
    amax = np.abs(w).max(1)
    if fmt == "e4m3":
        byte = np.frexp(amax)[1] - 1 + 127 - 7
    else:
        mant, ex = np.frexp(amax / 6.0)
        byte = np.where(mant > 0.5, ex, ex - 1) + 127
    byte = np.clip(np.where(amax > 0, byte, 1), 1, 254)
    scaled = (w * np.exp2(127.0 - byte)[:, None, :]).reshape(k, n).astype(np.float32)
    by_word = np.ascontiguousarray(scaled.reshape(k // 512, 128, 4, n).transpose(0, 1, 3, 2))
    if fmt == "e4m3":
        words = by_word.astype(ml_dtypes.float8_e4m3fn).view(np.uint8)
    else:
        c = by_word.astype(ml_dtypes.float4_e2m1fn).view(np.uint8) & 0xF
        words = (c[..., 0::2] | (c[..., 1::2] << 4)).reshape(k // 512, 128, 2 * n)
    return np.ascontiguousarray(words), np.ascontiguousarray(byte.astype(np.uint8).reshape(k // 512, 16, n))


def unpack_weight(words, scales, fmt):
    g, _, n = scales.shape
    words = np.ascontiguousarray(words).reshape(g, 128, n, -1)
    if fmt == "e4m3":
        vals = words.view(ml_dtypes.float8_e4m3fn).astype(np.float64)
    else:
        nib = np.empty((g, 128, n, 4), np.uint8)
        nib[..., 0::2] = words & 0xF
        nib[..., 1::2] = words >> 4
        vals = E2M1[nib]
    vals = vals * np.repeat(np.exp2(scales.astype(np.float64) - 127.0), 8, axis=1)[..., None]
    return vals.transpose(0, 1, 3, 2).reshape(g * 512, n)


def gelu(v):
    return 0.5 * v * (1.0 + np.tanh(np.sqrt(2.0 / np.pi) * (v + 0.044715 * v**3)))


K, T, S, T2, P, R, H, N = 1024, 4096, 1024, 2048, 512, 512, 1024, 512

def setup_inputs():
    n = np.random.standard_normal
    s = mx_kscale(K)[:, None]
    u = mx_kscale(H)[:, None]
    tab_words, tab_scales = pack_weight(n((K, T)) * s, "e4m3")
    tab2_words, tab2_scales = pack_weight(n((K, T2)) * s, "e4m3")
    w2_words, w2_scales = pack_weight(0.7 * n((K, R)) / np.sqrt(K) / s, "e2m1")
    w4_words, w4_scales = pack_weight(0.58 * n((K, N)) / np.sqrt(K) / s, "e4m3")
    gain = np.concatenate([np.random.uniform(2.5, 3.5, R), np.random.uniform(0.6, 1.0, H - R)])
    return {
        "tab_words": tab_words, "tab_scales": tab_scales,
        "tab2_words": tab2_words, "tab2_scales": tab2_scales,
        "offs": striped(np.random.permutation(T)[:S]),
        "offs2": striped(np.random.permutation(T2)[:P]),
        "pos1": striped(np.random.permutation(S)[:P]),
        "w1": (0.58 * n((K, R)) / np.sqrt(K) / s).astype(np.float32),
        "w2_words": w2_words, "w2_scales": w2_scales,
        "gain": (gain * u[:, 0]).astype(np.float32),
        "w3": (n((H, N)) / np.sqrt(H) / u).astype(np.float32),
        "w4_words": w4_words, "w4_scales": w4_scales,
        "w5": (0.5 * n((K, N)) / np.sqrt(K) / s).astype(np.float32),
    }

def reference(tab_words, tab_scales, tab2_words, tab2_scales, offs, offs2, pos1,
              w1, w2_words, w2_scales, gain, w3, w4_words, w4_scales, w5):
    v = unpack_weight(tab_words, tab_scales, "e4m3")[:, unstriped(offs)]
    v2 = unpack_weight(tab2_words, tab2_scales, "e4m3")[:, unstriped(offs2)]
    w2 = unpack_weight(w2_words, w2_scales, "e2m1")
    w4 = unpack_weight(w4_words, w4_scales, "e4m3")
    hs = np.sin(mxq(f64(w1), 0, "e4m3").T @ v)
    he = np.exp(w2.T @ v)
    h = f64(gain)[:, None] * np.concatenate([hs, he])
    d = np.tanh(mxq(f64(w3), 0, "e4m3").T @ mxq(h, 0, "e4m3"))
    y = d * np.cos(w4.T @ v)
    b = mxq(f64(w5), 0, "e4m3").T @ v2
    return y[:, unstriped(pos1)] + b

@@ -1,0 +1,370 @@
+import math
+from contextlib import ExitStack
+
+import concourse.mybir as mybir
+from concourse.masks import make_identity
+
+K, T, S, T2, TRIALS, R, H, N = 1024, 4096, 1024, 2048, 512, 512, 1024, 512
+FLOPS = 2 * K * S * (R + (H - R) + N) + 2 * H * N * S + 2 * K * N * TRIALS
+
+F32 = mybir.dt.float32
+BF16 = mybir.dt.bfloat16
+I32 = mybir.dt.int32
+U32 = mybir.dt.uint32
+U16 = mybir.dt.uint16
+U8 = mybir.dt.uint8
+FP8X4 = mybir.dt.float8_e4m3fn_x4
+FP4X4 = mybir.dt.float4_e2m1fn_x4
+ACT = mybir.ActivationFunctionType
+MULT = mybir.AluOpType.mult
+ADD = mybir.AluOpType.add
+SUB = mybir.AluOpType.subtract
+
+P = 128
+PACK = 4
+K_PASS = P * PACK
+PASSES = 2
+BANK = 512
+CHUNK = 128
+HALVES = S // BANK
+TWO_PI = 2.0 * math.pi
+KC, KS = "vector", "vector"
+CAST1, CAST3, CAST5 = "vector", "scalar", "scalar"
+LEAD = 8
+
+
+def tile_list_cartilage_wear_scores_kernel(
+    tc, tab_words, tab_scales, tab2_words, tab2_scales, offs, offs2, pos1,
+    w1, w2_words, w2_scales, gain, w3, w4_words, w4_scales, w5, out,
+):
+    nc = tc.nc
+    with ExitStack() as ctx:
+        lists = ctx.enter_context(tc.tile_pool(name="lists", bufs=1))
+        keep = ctx.enter_context(tc.tile_pool(name="keep", bufs=1))
+        stage = ctx.enter_context(tc.tile_pool(name="stage", bufs=1))
+        ring = ctx.enter_context(tc.tile_pool(name="ring", bufs=4))
+        psum = ctx.enter_context(tc.psum_pool(name="psum", bufs=7))
+        psum_gain = ctx.enter_context(tc.psum_pool(name="psum_gain", bufs=1))
+
+        def load_scale_rows(queue, tile, scales):
+            for q in range(4):
+                queue.dma_start(
+                    out=tile[32 * q : 32 * q + 4, :, :].bitcast(I32),
+                    in_=scales[:, 4 * q : 4 * q + 4, :].rearrange("a r n -> r a n").bitcast(I32),
+                )
+
+        def load_packed_rows(queue, tile, scales):
+            for q in range(4):
+                queue.dma_start(out=tile[32 * q : 32 * q + 8, :].bitcast(I32), in_=scales[:, 4 * q : 4 * q + 4, :].bitcast(I32))
+
+        def cast(engine, dst, src):
+            if engine == "vector":
+                nc.vector.tensor_copy(out=dst, in_=src)
+            elif engine == "scalar":
+                nc.scalar.copy(out=dst, in_=src)
+            else:
+                nc.gpsimd.tensor_scalar(out=dst, in0=src, scalar1=1.0, scalar2=0.0, op0=MULT, op1=ADD)
+
+        idx = lists.tile([P, S // 16], U16, name="idx")
+        idx2 = lists.tile([P, TRIALS // 16], U16, name="idx2")
+        picks = lists.tile([P, TRIALS // 16], U16, name="picks")
+        nc.sync.dma_start(idx[:], offs)
+        nc.sync.dma_start(idx2[:], offs2)
+        nc.sync.dma_start(picks[:], pos1)
+
+        tab_sc = stage.tile([P, T], U8, name="tab_sc", tag="s0", align_bytes=64)
+        nc.vector.memset(tab_sc[:].bitcast(I32), 0)
+        load_packed_rows(nc.scalar, tab_sc, tab_scales)
+        tab_w = []
+        for a in range(PASSES):
+            tile = stage.tile([P, T], U32, name="tab_w%d" % a, tag="s%d" % (1 + a), align_bytes=64)
+            nc.sync.dma_start(out=tile[:].bitcast(I32), in_=tab_words[a].rearrange("p t i -> p (t i)").bitcast(I32))
+            tab_w.append(tile)
+        w4_w = keep.tile([P, PASSES, N], U32, name="w4_w", align_bytes=64)
+        nc.sync.dma_start(out=w4_w[:].bitcast(I32), in_=w4_words.rearrange("a p c i -> p a (c i)").bitcast(I32))
+        w4_sc = keep.tile([P, N], U8, name="w4_sc", align_bytes=64)
+        nc.gpsimd.memset(w4_sc[:].bitcast(I32), 0)
+        for q in range(4):
+            queue = nc.gpsimd
+            queue.dma_start(out=w4_sc[32 * q : 32 * q + 8, :].bitcast(I32), in_=w4_scales[:, 4 * q : 4 * q + 4, :].bitcast(I32))
+
+        gain_rows = stage.tile([P, P], F32, name="gain_rows", tag="s5", align_bytes=64)
+        ident = stage.tile([P, P], F32, name="ident", tag="s6", align_bytes=64)
+        nc.gpsimd.memset(gain_rows[:], 0.0)
+        for b in range(PASSES):
+            nc.gpsimd.dma_start(
+                out=gain_rows[PACK * b : PACK * (b + 1), :].rearrange("t (q i) -> t q i", i=8),
+                in_=gain[K_PASS * b : K_PASS * (b + 1)].rearrange("(q t i) -> t q i", t=PACK, i=8),
+            )
+        make_identity(nc, ident[:])
+        gain_ps = psum_gain.tile([P, P], F32, name="gain_ps")
+        nc.tensor.transpose(gain_ps[:], gain_rows[:], ident[:])
+
+        w2_sc_raw = keep.tile([P, PASSES, R], U8, name="w2_sc_raw", align_bytes=64)
+        nc.gpsimd.memset(w2_sc_raw[:].rearrange("p a n -> p (a n)").bitcast(I32), 0)
+        load_scale_rows(nc.gpsimd, w2_sc_raw, w2_scales)
+        v_sc_low = keep.tile([P, S], U8, name="v_sc_low", align_bytes=64)
+        nc.gpsimd.memset(v_sc_low[:].bitcast(I32), 0)
+
+        v_w = [keep.tile([P, S], U32, name="v_w0", align_bytes=64)]
+        for half in range(HALVES):
+            nc.vector.tensor_copy(out=v_w[0][:, BANK * half : BANK * (half + 1)], in_=tab_w[0][:].indirect(idx[:, 32 * half : 32 * (half + 1)]))
+        v_sc = keep.tile([P, S], U8, name="v_sc", align_bytes=64)
+        nc.vector.tensor_copy(out=v_sc[:], in_=tab_sc[:].indirect(idx[:]))
+        v_w.append(stage.tile([P, S], U32, name="v_w1", tag="s0", align_bytes=64))
+        for half in range(HALVES):
+            nc.vector.tensor_copy(out=v_w[1][:, BANK * half : BANK * (half + 1)], in_=tab_w[1][:].indirect(idx[:, 32 * half : 32 * (half + 1)]))
+        w1_raw = stage.tile([P, PASSES, PACK, R], F32, name="w1_raw", tag="s1", align_bytes=64)
+        for a in range(PASSES):
+            nc.sync.dma_start(out=w1_raw[:, a], in_=w1[K_PASS * a : K_PASS * (a + 1), :].rearrange("(p j) c -> p j c", j=PACK))
+        late_raw = stage.tile([P, 2, PASSES, PACK, N], F32, name="late_raw", tag="s2", align_bytes=64)
+        w3_raw, w5_raw = late_raw[:, 0], late_raw[:, 1]
+        for b in range(PASSES):
+            rows = w3[K_PASS * b : K_PASS * (b + 1), :].rearrange("(q t i) n -> t q i n", t=PACK, i=8)
+            for t in range(PACK):
+                nc.sync.dma_start(out=w3_raw[:, b, t, :], in_=rows[t])
+        for a in range(PASSES):
+            nc.sync.dma_start(out=w5_raw[:, a], in_=w5[K_PASS * a : K_PASS * (a + 1), :].rearrange("(p j) c -> p j c", j=PACK))
+        w2_raw = stage.tile([P, PASSES, 2 * R], U8, name="w2_raw", tag="s5", align_bytes=64)
+        nc.sync.dma_start(out=w2_raw[:].bitcast(I32), in_=w2_words.rearrange("a p n -> p a n").bitcast(I32))
+        for q in range(4):
+            nc.sync.dma_start(out=v_sc_low[32 * q : 32 * q + 4, :].bitcast(I32), in_=v_sc[32 * q + 4 : 32 * q + 8, :].bitcast(I32))
+        tab2_sc = stage.tile([P, T2], U8, name="tab2_sc", tag="s6", align_bytes=64)
+        nc.gpsimd.memset(tab2_sc[:].bitcast(I32), 0)
+        load_packed_rows(nc.sync, tab2_sc, tab2_scales)
+
+        def quantize(codes, scales, grouped):
+            nc.vector.quantize_mx(out=codes.bitcast(FP8X4), scales=scales, in_=grouped)
+
+        def new_codes(name, width):
+            codes = keep.tile([P, width], U32, name=name + "_w", align_bytes=64)
+            scales = keep.tile([P, width], U8, name=name + "_sc", align_bytes=64)
+            return codes, scales
+
+        h_bf = {}
+        h_q = {}
+        for b in range(PASSES):
+            for half in range(HALVES):
+                h_bf[b, half] = keep.tile([P, BANK * PACK], BF16, name="h_bf%d%d" % (b, half), align_bytes=64)
+                h_q[b, half] = new_codes("h%d%d" % (b, half), BANK)
+
+        def first_stage_chunk(chunk, lhs_of, plane_of):
+            cols = slice(chunk * CHUNK, (chunk + 1) * CHUNK)
+            acc = psum.tile([P, PACK, CHUNK], F32, name="acc", tag="acc")
+            for t in range(PACK):
+                for a in range(PASSES):
+                    lhs, lhs_sc = lhs_of(a, t)
+                    nc.tensor.matmul_mx(
+                        out=acc[:, t, :], lhsT=lhs, lhsT_scale=lhs_sc,
+                        rhs=v_w[a][:, cols].bitcast(FP8X4), rhs_scale=plane_of(a, cols),
+                        start=(a == 0), stop=(a == PASSES - 1),
+                    )
+            return acc[:].rearrange("p t n -> p n t")
+
+        def scale_by_gain(b, chunk, values):
+            half, col = divmod(chunk * CHUNK, BANK)
+            nc.vector.tensor_tensor(
+                out=h_bf[b, half][:, PACK * col : PACK * (col + CHUNK)].rearrange("p (n t) -> p n t", t=PACK),
+                in0=values.rearrange("p (n t) -> p n t", t=PACK),
+                in1=gain_ps[:, PACK * b : PACK * (b + 1)].unsqueeze(1).to_broadcast([P, CHUNK, PACK]),
+                op=MULT,
+            )
+            if chunk % 2 == 1:
+                lo = col - CHUNK
+                codes, scales = h_q[b, half]
+                quantize(codes[:, lo : lo + 2 * CHUNK], scales[:, lo : lo + 2 * CHUNK],
+                         h_bf[b, half][:, PACK * lo : PACK * (lo + 2 * CHUNK)])
+
+        rests = stage.tile([P, 4, BANK], F32, name="rests", tag="s7", align_bytes=64)
+        wholes = stage.tile([P, 4, BANK], I32, name="wholes", tag="s8", align_bytes=64)
+
+        def quantize_weight(name, raw, engine):
+            grouped = ring.tile([P, PACK * N], BF16, name="grouped", align_bytes=64, bufs=2)
+            width = N // 4
+            for lo in range(0, N, width):
+                cast(engine, grouped[:, PACK * lo : PACK * (lo + width)].rearrange("p (c i j) -> p c j i", i=4, j=PACK),
+                     raw[:, :, lo : lo + width].rearrange("p j (c i) -> p c j i", i=4))
+            codes, scales = new_codes(name, N)
+            quantize(codes[:], scales[:], grouped[:])
+            return codes, scales
+
+        def product(lhs_of, rhs_of):
+            acc = psum.tile([P, BANK], F32, name="acc", tag="acc")
+            for a in range(PASSES):
+                lhs, lhs_sc = lhs_of(a)
+                rhs, rhs_sc = rhs_of(a)
+                nc.tensor.matmul_mx(out=acc[:], lhsT=lhs, lhsT_scale=lhs_sc, rhs=rhs, rhs_scale=rhs_sc,
+                                    start=(a == 0), stop=(a == PASSES - 1))
+            return acc
+
+        cosines = [keep.tile([P, S], F32, name="cos%d" % n) for n in range(N // P)]
+
+        w1_q, w3_q, w5_q = [], [], []
+
+        def quantize_w1(a):
+            grouped = stage.tile([P, PACK * R], BF16, name="w1_grouped%d" % a, tag="w1_grouped%d" % a, align_bytes=64)
+            for t in range(PACK):
+                cast(CAST1,
+                     grouped[:, R * t : R * (t + 1)].rearrange("p (q g i j) -> p q g j i", g=2, i=4, j=PACK),
+                     w1_raw[:, a].rearrange("p j (q t g i) -> p t q g j i", t=PACK, g=2, i=4)[:, t])
+            codes, scales = new_codes("w1_%d" % a, R)
+            quantize(codes[:], scales[:], grouped[:])
+            w1_q.append((codes, scales))
+
+        def w1_of(a, t):
+            codes, scales = w1_q[a]
+            return (codes[:, P * t : P * (t + 1)].bitcast(FP8X4), scales[:, P * t : P * (t + 1)])
+
+        def woven(ap):
+            return ap.rearrange("p (n t) -> p n t", t=PACK)
+
+        jobs = [("cos", n, half) for half in range(HALVES) for n in range(N // P)]
+        sines = [("sin", chunk, 0) for chunk in range(S // CHUNK)]
+        tail = jobs[LEAD:]
+        jobs = jobs[:LEAD]
+        for chunk in range(S // CHUNK):
+            jobs.append(sines[chunk])
+            if chunk < len(tail):
+                jobs.append(tail[chunk])
+        state = [dict() for job in jobs]
+
+        holds = {2: "w1_grouped0", 4: "w1_grouped1", 15: "v2_sc"}
+
+        def multiply(j):
+            kind, n, half = jobs[j]
+            if kind == "cos":
+                cols = slice(BANK * half, BANK * (half + 1))
+                acc = product(
+                    lambda a: (w4_w[:, a, P * n : P * (n + 1)].bitcast(FP8X4), w4_sc[4 * a : P, P * n : P * (n + 1)]),
+                    lambda a: (v_w[a][:, cols].bitcast(FP8X4), v_sc[4 * a : P, cols]),
+                )
+                state[j]["x"] = acc[:]
+            else:
+                state[j]["x"] = first_stage_chunk(n, w1_of, lambda a, cols: v_sc[4 * a : P, cols])
+
+        def engine_of(j):
+            return KC if jobs[j][0] == "cos" else KS
+
+        def to_turns(j):
+            if engine_of(j) == "direct":
+                return
+            if j in holds:
+                turns = stage.tile([P, BANK], F32, name="turns%d" % j, tag=holds[j], align_bytes=64)
+            else:
+                turns = ring.tile([P, BANK], F32, name="turns", bufs=4)
+            state[j]["turns"] = turns
+            if jobs[j][0] == "cos":
+                nc.scalar.activation(out=turns[:], in_=state[j]["x"], func=ACT.Copy, scale=1.0 / TWO_PI, bias=0.25)
+            else:
+                nc.scalar.activation(out=woven(turns[:]), in_=state[j]["x"], func=ACT.Copy, scale=1.0 / TWO_PI)
+
+        def round_turns(j):
+            whole = wholes[:, j % 4]
+            if engine_of(j) == "direct":
+                nc.vector.tensor_scalar(out=woven(whole), in0=state[j]["x"], scalar1=1.0 / TWO_PI, scalar2=None, op0=MULT)
+            elif engine_of(j) == "gpsimd":
+                nc.gpsimd.tensor_scalar(out=whole, in0=state[j]["turns"][:], scalar1=1.0, scalar2=0.0, op0=MULT, op1=ADD)
+            else:
+                nc.vector.tensor_copy(out=whole, in_=state[j]["turns"][:])
+
+        def take_rest(j):
+            whole, rest = wholes[:, j % 4], rests[:, j % 4]
+            if jobs[j][0] == "cos" or False:
+                nc.vector.tensor_tensor(out=rest, in0=state[j]["turns"][:], in1=whole, op=SUB)
+            else:
+                nc.vector.scalar_tensor_tensor(out=woven(rest), in0=state[j]["x"], scalar=1.0 / TWO_PI, in1=woven(whole), op0=MULT, op1=SUB)
+
+        def sine(j):
+            kind, n, half = jobs[j]
+            if kind == "cos":
+                dst = cosines[n][:, BANK * half : BANK * (half + 1)]
+            else:
+                values = ring.tile([P, BANK], F32, name="values", bufs=4)
+                dst = values[:]
+                state[j]["values"] = dst
+            nc.scalar.activation(out=dst, in_=rests[:, j % 4], func=ACT.Sin, scale=TWO_PI)
+
+        def finish(j):
+            if jobs[j][0] == "sin":
+                scale_by_gain(0, jobs[j][1], state[j]["values"])
+
+        steps = (multiply, to_turns, round_turns, take_rest, sine, finish)
+        lags = (0, 1, 2, 4, 5, 7)
+        for step in range(len(jobs) + lags[-1]):
+            if step in (7, 7 + 1):
+                quantize_w1(len(w1_q))
+                if len(w1_q) == PASSES:
+                    tab2_w = stage.tile([P, PASSES, T2], U32, name="tab2_w", tag="s1", align_bytes=64)
+                    for a in range(PASSES):
+                        nc.sync.dma_start(out=tab2_w[:, a, :].bitcast(I32), in_=tab2_words[a].rearrange("p t i -> p (t i)").bitcast(I32))
+            for work, lag in zip(steps, lags):
+                if 0 <= step - lag < len(jobs):
+                    work(step - lag)
+            if step in (9, 9 + 3):
+                w3_q.append(quantize_weight("w3_%d" % len(w3_q), w3_raw[:, len(w3_q)], CAST3))
+
+        w2_w = keep.tile([P, PASSES, 2 * R], U8, name="w2_w", align_bytes=64)
+        nc.vector.tensor_copy(
+            out=w2_w[:].bitcast(I32).rearrange("p a (t q w) -> p a t q w", t=PACK, w=4),
+            in_=w2_raw[:].bitcast(I32).rearrange("p a (q t w) -> p a t q w", t=PACK, w=4),
+        )
+        w2_sc = keep.tile([P, PASSES, R], U8, name="w2_sc", align_bytes=64)
+        nc.vector.tensor_copy(
+            out=w2_sc[:].bitcast(I32).rearrange("p a (t q w) -> p a t q w", t=PACK, w=2),
+            in_=w2_sc_raw[:].bitcast(I32).rearrange("p a (q t w) -> p a t q w", t=PACK, w=2),
+        )
+
+
+        def w2_of(a, t):
+            return (w2_w[:, a, 2 * P * t : 2 * P * (t + 1)].bitcast(FP4X4), w2_sc[:, a, P * t : P * (t + 1)])
+
+        exps = stage.tile([P, 4, BANK], F32, name="exps", tag="s7", align_bytes=64)
+
+        def exp_chunk(chunk):
+            x = first_stage_chunk(chunk, w2_of, lambda a, cols: (v_sc, v_sc_low)[a][:, cols])
+            values = exps[:, chunk % 4]
+            nc.scalar.activation(out=values.rearrange("p (n t) -> p n t", t=PACK), in_=x, func=ACT.Exp)
+
+        own = []
+
+        def own_bank(n):
+            acc = product(
+                lambda a: (w5_q[a][0][:, P * n : P * (n + 1)].bitcast(FP8X4), w5_q[a][1][:, P * n : P * (n + 1)]),
+                lambda a: (v2_w[:, a, :].bitcast(FP8X4), v2_sc[4 * a : P, :]),
+            )
+            tile = keep.tile([P, TRIALS], F32, name="own%d" % n)
+            nc.scalar.copy(out=tile[:], in_=acc[:])
+            own.append(tile)
+
+        scores = [keep.tile([P, S], F32, name="y%d" % n) for n in range(N // P)]
+
+        def second_stage(n, half):
+            acc = product(
+                lambda b: (w3_q[b][0][:, P * n : P * (n + 1)].bitcast(FP8X4), w3_q[b][1][:, P * n : P * (n + 1)]),
+                lambda b: (h_q[b, half][0][:].bitcast(FP8X4), h_q[b, half][1][:]),
+            )
+            d = ring.tile([P, BANK], F32, name="d", bufs=3)
+            nc.scalar.activation(out=d[:], in_=acc[:], func=ACT.Tanh)
+            cols = slice(BANK * half, BANK * (half + 1))
+            nc.vector.tensor_tensor(out=scores[n][:, cols], in0=d[:], in1=cosines[n][:, cols], op=MULT)
+
+        v2_sc = stage.tile([P, TRIALS], U8, name="v2_sc", tag="v2_sc", align_bytes=64)
+        nc.vector.tensor_copy(out=v2_sc[:], in_=tab2_sc[:].indirect(idx2[:]))
+        v2_w = stage.tile([P, PASSES, TRIALS], U32, name="v2_w", tag="s8", align_bytes=64)
+        for a in range(PASSES):
+            nc.vector.tensor_copy(out=v2_w[:, a, :], in_=tab2_w[:, a, :].indirect(idx2[:]))
+        for chunk in range(S // CHUNK + 2):
+            if chunk < S // CHUNK:
+                exp_chunk(chunk)
+            if chunk >= 2:
+                scale_by_gain(1, chunk - 2, exps[:, (chunk - 2) % 4])
+            if chunk in (3, 3 + 4):
+                w5_q.append(quantize_weight("w5_%d" % len(w5_q), w5_raw[:, len(w5_q)], CAST5))
+        for n in range(N // P):
+            second_stage(n, 0)
+        for n in range(N // P):
+            second_stage(n, 1)
+            own_bank(n)
+            result = ring.tile([P, TRIALS], F32, name="result")
+            nc.vector.tensor_tensor(out=result[:], in0=scores[n][:].indirect(picks[:]), in1=own[n][:], op=ADD)
+            nc.sync.dma_start(out=out[P * n : P * (n + 1), :], in_=result[:])

@@ -26,11 +26,11 @@ K_PASS = P * PACK
 PASSES = 2
 BANK = 512
 CHUNK = 128
+PAIR = 2
+WIDE = PAIR * BANK
 HALVES = S // BANK
+TILES = N // P
 TWO_PI = 2.0 * math.pi
-KC, KS = "vector", "vector"
-CAST1, CAST3, CAST5 = "vector", "scalar", "scalar"
-LEAD = 8
 
 
 def tile_list_cartilage_wear_scores_kernel(
@@ -42,16 +42,9 @@ def tile_list_cartilage_wear_scores_kernel(
         lists = ctx.enter_context(tc.tile_pool(name="lists", bufs=1))
         keep = ctx.enter_context(tc.tile_pool(name="keep", bufs=1))
         stage = ctx.enter_context(tc.tile_pool(name="stage", bufs=1))
-        ring = ctx.enter_context(tc.tile_pool(name="ring", bufs=4))
+        ring = ctx.enter_context(tc.tile_pool(name="ring", bufs=2))
         psum = ctx.enter_context(tc.psum_pool(name="psum", bufs=7))
         psum_gain = ctx.enter_context(tc.psum_pool(name="psum_gain", bufs=1))
-
-        def load_scale_rows(queue, tile, scales):
-            for q in range(4):
-                queue.dma_start(
-                    out=tile[32 * q : 32 * q + 4, :, :].bitcast(I32),
-                    in_=scales[:, 4 * q : 4 * q + 4, :].rearrange("a r n -> r a n").bitcast(I32),
-                )
 
         def load_packed_rows(queue, tile, scales):
             for q in range(4):
@@ -84,9 +77,7 @@ def tile_list_cartilage_wear_scores_kernel(
         nc.sync.dma_start(out=w4_w[:].bitcast(I32), in_=w4_words.rearrange("a p c i -> p a (c i)").bitcast(I32))
         w4_sc = keep.tile([P, N], U8, name="w4_sc", align_bytes=64)
         nc.gpsimd.memset(w4_sc[:].bitcast(I32), 0)
-        for q in range(4):
-            queue = nc.gpsimd
-            queue.dma_start(out=w4_sc[32 * q : 32 * q + 8, :].bitcast(I32), in_=w4_scales[:, 4 * q : 4 * q + 4, :].bitcast(I32))
+        load_packed_rows(nc.gpsimd, w4_sc, w4_scales)
 
         gain_rows = stage.tile([P, P], F32, name="gain_rows", tag="s5", align_bytes=64)
         ident = stage.tile([P, P], F32, name="ident", tag="s6", align_bytes=64)
@@ -102,13 +93,19 @@ def tile_list_cartilage_wear_scores_kernel(
 
         w2_sc_raw = keep.tile([P, PASSES, R], U8, name="w2_sc_raw", align_bytes=64)
         nc.gpsimd.memset(w2_sc_raw[:].rearrange("p a n -> p (a n)").bitcast(I32), 0)
-        load_scale_rows(nc.gpsimd, w2_sc_raw, w2_scales)
+        for q in range(4):
+            nc.gpsimd.dma_start(
+                out=w2_sc_raw[32 * q : 32 * q + 4, :, :].bitcast(I32),
+                in_=w2_scales[:, 4 * q : 4 * q + 4, :].rearrange("a r n -> r a n").bitcast(I32),
+            )
         v_sc_low = keep.tile([P, S], U8, name="v_sc_low", align_bytes=64)
         nc.gpsimd.memset(v_sc_low[:].bitcast(I32), 0)
+        tab2_sc = keep.tile([P, T2], U8, name="tab2_sc", align_bytes=64)
+        nc.gpsimd.memset(tab2_sc[:].bitcast(I32), 0)
+        load_packed_rows(nc.gpsimd, tab2_sc, tab2_scales)
 
         v_w = [keep.tile([P, S], U32, name="v_w0", align_bytes=64)]
-        for half in range(HALVES):
-            nc.vector.tensor_copy(out=v_w[0][:, BANK * half : BANK * (half + 1)], in_=tab_w[0][:].indirect(idx[:, 32 * half : 32 * (half + 1)]))
+        nc.vector.tensor_copy(out=v_w[0][:], in_=tab_w[0][:].indirect(idx[:]))
         v_sc = keep.tile([P, S], U8, name="v_sc", align_bytes=64)
         nc.vector.tensor_copy(out=v_sc[:], in_=tab_sc[:].indirect(idx[:]))
         v_w.append(stage.tile([P, S], U32, name="v_w1", tag="s0", align_bytes=64))
@@ -129,26 +126,36 @@ def tile_list_cartilage_wear_scores_kernel(
         nc.sync.dma_start(out=w2_raw[:].bitcast(I32), in_=w2_words.rearrange("a p n -> p a n").bitcast(I32))
         for q in range(4):
             nc.sync.dma_start(out=v_sc_low[32 * q : 32 * q + 4, :].bitcast(I32), in_=v_sc[32 * q + 4 : 32 * q + 8, :].bitcast(I32))
-        tab2_sc = stage.tile([P, T2], U8, name="tab2_sc", tag="s6", align_bytes=64)
-        nc.gpsimd.memset(tab2_sc[:].bitcast(I32), 0)
-        load_packed_rows(nc.sync, tab2_sc, tab2_scales)
 
-        def quantize(codes, scales, grouped):
-            nc.vector.quantize_mx(out=codes.bitcast(FP8X4), scales=scales, in_=grouped)
-
-        def new_codes(name, width):
-            codes = keep.tile([P, width], U32, name=name + "_w", align_bytes=64)
-            scales = keep.tile([P, width], U8, name=name + "_sc", align_bytes=64)
+        def quantize(name, grouped):
+            codes = keep.tile([P, N], U32, name=name + "_w", align_bytes=64)
+            scales = keep.tile([P, N], U8, name=name + "_sc", align_bytes=64)
+            nc.vector.quantize_mx(out=codes[:].bitcast(FP8X4), scales=scales[:], in_=grouped[:])
             return codes, scales
 
-        h_bf = {}
-        h_q = {}
-        for b in range(PASSES):
-            for half in range(HALVES):
-                h_bf[b, half] = keep.tile([P, BANK * PACK], BF16, name="h_bf%d%d" % (b, half), align_bytes=64)
-                h_q[b, half] = new_codes("h%d%d" % (b, half), BANK)
+        def quantize_weight(name, raw, engine):
+            grouped = ring.tile([P, PACK * N], BF16, name="grouped", align_bytes=64)
+            width = N // 2
+            for lo in range(0, N, width):
+                cast(engine, grouped[:, PACK * lo : PACK * (lo + width)].rearrange("p (c i j) -> p c j i", i=4, j=PACK),
+                     raw[:, :, lo : lo + width].rearrange("p j (c i) -> p c j i", i=4))
+            return quantize(name, grouped)
 
-        def first_stage_chunk(chunk, lhs_of, plane_of):
+        def quantize_w1(a):
+            grouped = stage.tile([P, PACK * R], BF16, name="w1_grouped%d" % a, tag="w1_grouped%d" % a, align_bytes=64)
+            cast("vector",
+                 grouped[:].rearrange("p (t q i j) -> p t q i j", t=PACK, i=8, j=PACK),
+                 w1_raw[:, a].rearrange("p j (q t i) -> p t q i j", t=PACK, i=8))
+            return quantize("w1_%d" % a, grouped)
+
+        h_bf = [keep.tile([P, S * PACK], BF16, name="h_bf%d" % b, align_bytes=64) for b in range(PASSES)]
+        h_w = [keep.tile([P, S], U32, name="h_w%d" % b, align_bytes=64) for b in range(PASSES)]
+        h_sc = [keep.tile([P, S], U8, name="h_sc%d" % b, align_bytes=64) for b in range(PASSES)]
+
+        def woven(ap):
+            return ap.rearrange("p (n t) -> p n t", t=PACK)
+
+        def feature_bank(chunk, lhs_of, plane_of):
             cols = slice(chunk * CHUNK, (chunk + 1) * CHUNK)
             acc = psum.tile([P, PACK, CHUNK], F32, name="acc", tag="acc")
             for t in range(PACK):
@@ -161,33 +168,6 @@ def tile_list_cartilage_wear_scores_kernel(
                     )
             return acc[:].rearrange("p t n -> p n t")
 
-        def scale_by_gain(b, chunk, values):
-            half, col = divmod(chunk * CHUNK, BANK)
-            nc.vector.tensor_tensor(
-                out=h_bf[b, half][:, PACK * col : PACK * (col + CHUNK)].rearrange("p (n t) -> p n t", t=PACK),
-                in0=values.rearrange("p (n t) -> p n t", t=PACK),
-                in1=gain_ps[:, PACK * b : PACK * (b + 1)].unsqueeze(1).to_broadcast([P, CHUNK, PACK]),
-                op=MULT,
-            )
-            if chunk % 2 == 1:
-                lo = col - CHUNK
-                codes, scales = h_q[b, half]
-                quantize(codes[:, lo : lo + 2 * CHUNK], scales[:, lo : lo + 2 * CHUNK],
-                         h_bf[b, half][:, PACK * lo : PACK * (lo + 2 * CHUNK)])
-
-        rests = stage.tile([P, 4, BANK], F32, name="rests", tag="s7", align_bytes=64)
-        wholes = stage.tile([P, 4, BANK], I32, name="wholes", tag="s8", align_bytes=64)
-
-        def quantize_weight(name, raw, engine):
-            grouped = ring.tile([P, PACK * N], BF16, name="grouped", align_bytes=64, bufs=2)
-            width = N // 4
-            for lo in range(0, N, width):
-                cast(engine, grouped[:, PACK * lo : PACK * (lo + width)].rearrange("p (c i j) -> p c j i", i=4, j=PACK),
-                     raw[:, :, lo : lo + width].rearrange("p j (c i) -> p c j i", i=4))
-            codes, scales = new_codes(name, N)
-            quantize(codes[:], scales[:], grouped[:])
-            return codes, scales
-
         def product(lhs_of, rhs_of):
             acc = psum.tile([P, BANK], F32, name="acc", tag="acc")
             for a in range(PASSES):
@@ -195,104 +175,91 @@ def tile_list_cartilage_wear_scores_kernel(
                 rhs, rhs_sc = rhs_of(a)
                 nc.tensor.matmul_mx(out=acc[:], lhsT=lhs, lhsT_scale=lhs_sc, rhs=rhs, rhs_scale=rhs_sc,
                                     start=(a == 0), stop=(a == PASSES - 1))
-            return acc
+            return acc[:]
 
-        cosines = [keep.tile([P, S], F32, name="cos%d" % n) for n in range(N // P)]
+        def scale_by_gain(b, pair, values):
+            nc.vector.tensor_tensor(
+                out=woven(h_bf[b][:, WIDE * pair : WIDE * (pair + 1)]),
+                in0=woven(values),
+                in1=gain_ps[:, PACK * b : PACK * (b + 1)].unsqueeze(1).to_broadcast([P, PAIR * CHUNK, PACK]),
+                op=MULT,
+            )
 
+        def quantize_h(b, pair):
+            cols = slice(PAIR * CHUNK * pair, PAIR * CHUNK * (pair + 1))
+            nc.vector.quantize_mx(out=h_w[b][:, cols].bitcast(FP8X4), scales=h_sc[b][:, cols],
+                                  in_=h_bf[b][:, WIDE * pair : WIDE * (pair + 1)])
+
+        cosines = keep.tile([P, HALVES * TILES * BANK], F32, name="cosines")
+        rests = stage.tile([P, 3, WIDE], F32, name="rests", tag="s7", align_bytes=64)
+        wholes = stage.tile([P, 3, WIDE], I32, name="wholes", tag="s8", align_bytes=64)
         w1_q, w3_q, w5_q = [], [], []
-
-        def quantize_w1(a):
-            grouped = stage.tile([P, PACK * R], BF16, name="w1_grouped%d" % a, tag="w1_grouped%d" % a, align_bytes=64)
-            for t in range(PACK):
-                cast(CAST1,
-                     grouped[:, R * t : R * (t + 1)].rearrange("p (q g i j) -> p q g j i", g=2, i=4, j=PACK),
-                     w1_raw[:, a].rearrange("p j (q t g i) -> p t q g j i", t=PACK, g=2, i=4)[:, t])
-            codes, scales = new_codes("w1_%d" % a, R)
-            quantize(codes[:], scales[:], grouped[:])
-            w1_q.append((codes, scales))
 
         def w1_of(a, t):
             codes, scales = w1_q[a]
             return (codes[:, P * t : P * (t + 1)].bitcast(FP8X4), scales[:, P * t : P * (t + 1)])
 
-        def woven(ap):
-            return ap.rearrange("p (n t) -> p n t", t=PACK)
-
-        jobs = [("cos", n, half) for half in range(HALVES) for n in range(N // P)]
-        sines = [("sin", chunk, 0) for chunk in range(S // CHUNK)]
-        tail = jobs[LEAD:]
-        jobs = jobs[:LEAD]
-        for chunk in range(S // CHUNK):
-            jobs.append(sines[chunk])
-            if chunk < len(tail):
-                jobs.append(tail[chunk])
+        jobs = [("cos", pair) for pair in range(4)] + [("sin", pair) for pair in range(4)]
         state = [dict() for job in jobs]
-
-        holds = {2: "w1_grouped0", 4: "w1_grouped1", 15: "v2_sc"}
+        holds = {0: "w1_grouped0", 1: "w1_grouped1", 7: "v2_sc"}
 
         def multiply(j):
-            kind, n, half = jobs[j]
-            if kind == "cos":
-                cols = slice(BANK * half, BANK * (half + 1))
-                acc = product(
-                    lambda a: (w4_w[:, a, P * n : P * (n + 1)].bitcast(FP8X4), w4_sc[4 * a : P, P * n : P * (n + 1)]),
-                    lambda a: (v_w[a][:, cols].bitcast(FP8X4), v_sc[4 * a : P, cols]),
-                )
-                state[j]["x"] = acc[:]
-            else:
-                state[j]["x"] = first_stage_chunk(n, w1_of, lambda a, cols: v_sc[4 * a : P, cols])
-
-        def engine_of(j):
-            return KC if jobs[j][0] == "cos" else KS
+            kind, pair = jobs[j]
+            banks = []
+            for bank in range(PAIR * pair, PAIR * (pair + 1)):
+                if kind == "cos":
+                    half, n = divmod(bank, TILES)
+                    cols = slice(BANK * half, BANK * (half + 1))
+                    banks.append(product(
+                        lambda a: (w4_w[:, a, P * n : P * (n + 1)].bitcast(FP8X4), w4_sc[4 * a : P, P * n : P * (n + 1)]),
+                        lambda a: (v_w[a][:, cols].bitcast(FP8X4), v_sc[4 * a : P, cols]),
+                    ))
+                else:
+                    banks.append(feature_bank(bank, w1_of, lambda a, cols: v_sc[4 * a : P, cols]))
+            state[j]["banks"] = banks
 
         def to_turns(j):
-            if engine_of(j) == "direct":
-                return
             if j in holds:
-                turns = stage.tile([P, BANK], F32, name="turns%d" % j, tag=holds[j], align_bytes=64)
+                turns = stage.tile([P, WIDE], F32, name="turns%d" % j, tag=holds[j], align_bytes=64)
             else:
-                turns = ring.tile([P, BANK], F32, name="turns", bufs=4)
+                turns = ring.tile([P, WIDE], F32, name="turns", bufs=3)
             state[j]["turns"] = turns
-            if jobs[j][0] == "cos":
-                nc.scalar.activation(out=turns[:], in_=state[j]["x"], func=ACT.Copy, scale=1.0 / TWO_PI, bias=0.25)
-            else:
-                nc.scalar.activation(out=woven(turns[:]), in_=state[j]["x"], func=ACT.Copy, scale=1.0 / TWO_PI)
+            for side, bank in enumerate(state[j]["banks"]):
+                dst = turns[:, BANK * side : BANK * (side + 1)]
+                if jobs[j][0] == "cos":
+                    nc.scalar.activation(out=dst, in_=bank, func=ACT.Copy, scale=1.0 / TWO_PI, bias=0.25)
+                else:
+                    nc.scalar.activation(out=woven(dst), in_=bank, func=ACT.Copy, scale=1.0 / TWO_PI)
 
         def round_turns(j):
-            whole = wholes[:, j % 4]
-            if engine_of(j) == "direct":
-                nc.vector.tensor_scalar(out=woven(whole), in0=state[j]["x"], scalar1=1.0 / TWO_PI, scalar2=None, op0=MULT)
-            elif engine_of(j) == "gpsimd":
-                nc.gpsimd.tensor_scalar(out=whole, in0=state[j]["turns"][:], scalar1=1.0, scalar2=0.0, op0=MULT, op1=ADD)
-            else:
-                nc.vector.tensor_copy(out=whole, in_=state[j]["turns"][:])
+            nc.vector.tensor_copy(out=wholes[:, j % 3], in_=state[j]["turns"][:])
 
         def take_rest(j):
-            whole, rest = wholes[:, j % 4], rests[:, j % 4]
-            if jobs[j][0] == "cos" or False:
-                nc.vector.tensor_tensor(out=rest, in0=state[j]["turns"][:], in1=whole, op=SUB)
-            else:
-                nc.vector.scalar_tensor_tensor(out=woven(rest), in0=state[j]["x"], scalar=1.0 / TWO_PI, in1=woven(whole), op0=MULT, op1=SUB)
+            nc.vector.tensor_tensor(out=rests[:, j % 3], in0=state[j]["turns"][:], in1=wholes[:, j % 3], op=SUB)
 
         def sine(j):
-            kind, n, half = jobs[j]
+            kind, pair = jobs[j]
             if kind == "cos":
-                dst = cosines[n][:, BANK * half : BANK * (half + 1)]
+                dst = cosines[:, WIDE * pair : WIDE * (pair + 1)]
             else:
-                values = ring.tile([P, BANK], F32, name="values", bufs=4)
+                values = ring.tile([P, WIDE], F32, name="values", bufs=2)
                 dst = values[:]
                 state[j]["values"] = dst
-            nc.scalar.activation(out=dst, in_=rests[:, j % 4], func=ACT.Sin, scale=TWO_PI)
+            nc.scalar.activation(out=dst, in_=rests[:, j % 3], func=ACT.Sin, scale=TWO_PI)
 
-        def finish(j):
+        def weigh(j):
             if jobs[j][0] == "sin":
                 scale_by_gain(0, jobs[j][1], state[j]["values"])
 
-        steps = (multiply, to_turns, round_turns, take_rest, sine, finish)
-        lags = (0, 1, 2, 4, 5, 7)
+        def finish(j):
+            if jobs[j][0] == "sin":
+                quantize_h(0, jobs[j][1])
+
+        steps = (multiply, to_turns, round_turns, take_rest, sine, weigh, finish)
+        lags = (0, 1, 2, 3, 4, 5, 6)
         for step in range(len(jobs) + lags[-1]):
-            if step in (7, 7 + 1):
-                quantize_w1(len(w1_q))
+            if step in (3, 3 + 1):
+                w1_q.append(quantize_w1(len(w1_q)))
                 if len(w1_q) == PASSES:
                     tab2_w = stage.tile([P, PASSES, T2], U32, name="tab2_w", tag="s1", align_bytes=64)
                     for a in range(PASSES):
@@ -300,8 +267,8 @@ def tile_list_cartilage_wear_scores_kernel(
             for work, lag in zip(steps, lags):
                 if 0 <= step - lag < len(jobs):
                     work(step - lag)
-            if step in (9, 9 + 3):
-                w3_q.append(quantize_weight("w3_%d" % len(w3_q), w3_raw[:, len(w3_q)], CAST3))
+            if step in (6, 6 + 2):
+                w3_q.append(quantize_weight("w3_%d" % len(w3_q), w3_raw[:, len(w3_q)], "scalar"))
 
         w2_w = keep.tile([P, PASSES, 2 * R], U8, name="w2_w", align_bytes=64)
         nc.vector.tensor_copy(
@@ -314,57 +281,52 @@ def tile_list_cartilage_wear_scores_kernel(
             in_=w2_sc_raw[:].bitcast(I32).rearrange("p a (q t w) -> p a t q w", t=PACK, w=2),
         )
 
-
         def w2_of(a, t):
             return (w2_w[:, a, 2 * P * t : 2 * P * (t + 1)].bitcast(FP4X4), w2_sc[:, a, P * t : P * (t + 1)])
-
-        exps = stage.tile([P, 4, BANK], F32, name="exps", tag="s7", align_bytes=64)
-
-        def exp_chunk(chunk):
-            x = first_stage_chunk(chunk, w2_of, lambda a, cols: (v_sc, v_sc_low)[a][:, cols])
-            values = exps[:, chunk % 4]
-            nc.scalar.activation(out=values.rearrange("p (n t) -> p n t", t=PACK), in_=x, func=ACT.Exp)
-
-        own = []
-
-        def own_bank(n):
-            acc = product(
-                lambda a: (w5_q[a][0][:, P * n : P * (n + 1)].bitcast(FP8X4), w5_q[a][1][:, P * n : P * (n + 1)]),
-                lambda a: (v2_w[:, a, :].bitcast(FP8X4), v2_sc[4 * a : P, :]),
-            )
-            tile = keep.tile([P, TRIALS], F32, name="own%d" % n)
-            nc.scalar.copy(out=tile[:], in_=acc[:])
-            own.append(tile)
-
-        scores = [keep.tile([P, S], F32, name="y%d" % n) for n in range(N // P)]
-
-        def second_stage(n, half):
-            acc = product(
-                lambda b: (w3_q[b][0][:, P * n : P * (n + 1)].bitcast(FP8X4), w3_q[b][1][:, P * n : P * (n + 1)]),
-                lambda b: (h_q[b, half][0][:].bitcast(FP8X4), h_q[b, half][1][:]),
-            )
-            d = ring.tile([P, BANK], F32, name="d", bufs=3)
-            nc.scalar.activation(out=d[:], in_=acc[:], func=ACT.Tanh)
-            cols = slice(BANK * half, BANK * (half + 1))
-            nc.vector.tensor_tensor(out=scores[n][:, cols], in0=d[:], in1=cosines[n][:, cols], op=MULT)
 
         v2_sc = stage.tile([P, TRIALS], U8, name="v2_sc", tag="v2_sc", align_bytes=64)
         nc.vector.tensor_copy(out=v2_sc[:], in_=tab2_sc[:].indirect(idx2[:]))
         v2_w = stage.tile([P, PASSES, TRIALS], U32, name="v2_w", tag="s8", align_bytes=64)
         for a in range(PASSES):
             nc.vector.tensor_copy(out=v2_w[:, a, :], in_=tab2_w[:, a, :].indirect(idx2[:]))
-        for chunk in range(S // CHUNK + 2):
-            if chunk < S // CHUNK:
-                exp_chunk(chunk)
-            if chunk >= 2:
-                scale_by_gain(1, chunk - 2, exps[:, (chunk - 2) % 4])
-            if chunk in (3, 3 + 4):
-                w5_q.append(quantize_weight("w5_%d" % len(w5_q), w5_raw[:, len(w5_q)], CAST5))
-        for n in range(N // P):
+
+        exps = stage.tile([P, 3, WIDE], F32, name="exps", tag="s7", align_bytes=64)
+        pairs = S // (PAIR * CHUNK)
+        for step in range(pairs + 2):
+            if step < pairs:
+                for side in range(PAIR):
+                    bank = feature_bank(PAIR * step + side, w2_of, lambda a, cols: (v_sc, v_sc_low)[a][:, cols])
+                    nc.scalar.activation(out=woven(exps[:, step % 3, BANK * side : BANK * (side + 1)]), in_=bank, func=ACT.Exp)
+            if 0 <= step - 1 < pairs:
+                scale_by_gain(1, step - 1, exps[:, (step - 1) % 3])
+            if 0 <= step - 2 < pairs:
+                quantize_h(1, step - 2)
+            if step in (0, 0 + 2):
+                w5_q.append(quantize_weight("w5_%d" % len(w5_q), w5_raw[:, len(w5_q)], "scalar"))
+
+        scores = [keep.tile([P, S], F32, name="y%d" % n) for n in range(TILES)]
+
+        def second_stage(n, half):
+            cols = slice(BANK * half, BANK * (half + 1))
+            acc = product(
+                lambda b: (w3_q[b][0][:, P * n : P * (n + 1)].bitcast(FP8X4), w3_q[b][1][:, P * n : P * (n + 1)]),
+                lambda b: (h_w[b][:, cols].bitcast(FP8X4), h_sc[b][:, cols]),
+            )
+            d = ring.tile([P, BANK], F32, name="d", bufs=3)
+            nc.scalar.activation(out=d[:], in_=acc, func=ACT.Tanh)
+            bank = TILES * half + n
+            nc.vector.tensor_tensor(out=scores[n][:, cols], in0=d[:], in1=cosines[:, BANK * bank : BANK * (bank + 1)], op=MULT)
+
+        for n in range(TILES):
             second_stage(n, 0)
-        for n in range(N // P):
+        for n in range(TILES):
             second_stage(n, 1)
-            own_bank(n)
+            acc = product(
+                lambda a: (w5_q[a][0][:, P * n : P * (n + 1)].bitcast(FP8X4), w5_q[a][1][:, P * n : P * (n + 1)]),
+                lambda a: (v2_w[:, a, :].bitcast(FP8X4), v2_sc[4 * a : P, :]),
+            )
+            own = ring.tile([P, TRIALS], F32, name="own", bufs=3)
+            nc.scalar.copy(out=own[:], in_=acc)
             result = ring.tile([P, TRIALS], F32, name="result")
-            nc.vector.tensor_tensor(out=result[:], in0=scores[n][:].indirect(picks[:]), in1=own[n][:], op=ADD)
+            nc.vector.tensor_tensor(out=result[:], in0=scores[n][:].indirect(picks[:]), in1=own[:], op=ADD)
             nc.sync.dma_start(out=out[P * n : P * (n + 1), :], in_=result[:])

@@ -43,8 +43,7 @@ def tile_list_cartilage_wear_scores_kernel(
         keep = ctx.enter_context(tc.tile_pool(name="keep", bufs=1))
         stage = ctx.enter_context(tc.tile_pool(name="stage", bufs=1))
         ring = ctx.enter_context(tc.tile_pool(name="ring", bufs=2))
-        psum = ctx.enter_context(tc.psum_pool(name="psum", bufs=7))
-        psum_gain = ctx.enter_context(tc.psum_pool(name="psum_gain", bufs=1))
+        psum = ctx.enter_context(tc.psum_pool(name="psum", bufs=8))
 
         def load_packed_rows(queue, tile, scales):
             for q in range(4):
@@ -65,9 +64,11 @@ def tile_list_cartilage_wear_scores_kernel(
         nc.sync.dma_start(idx2[:], offs2)
         nc.sync.dma_start(picks[:], pos1)
 
+        ident = keep.tile([P, P], F32, name="ident")
+        make_identity(nc, ident[:])
         tab_sc = stage.tile([P, T], U8, name="tab_sc", tag="s0", align_bytes=64)
         nc.vector.memset(tab_sc[:].bitcast(I32), 0)
-        load_packed_rows(nc.scalar, tab_sc, tab_scales)
+        load_packed_rows(nc.gpsimd, tab_sc, tab_scales)
         tab_w = []
         for a in range(PASSES):
             tile = stage.tile([P, T], U32, name="tab_w%d" % a, tag="s%d" % (1 + a), align_bytes=64)
@@ -75,34 +76,23 @@ def tile_list_cartilage_wear_scores_kernel(
             tab_w.append(tile)
         w4_w = keep.tile([P, PASSES, N], U32, name="w4_w", align_bytes=64)
         nc.sync.dma_start(out=w4_w[:].bitcast(I32), in_=w4_words.rearrange("a p c i -> p a (c i)").bitcast(I32))
-        w4_sc = keep.tile([P, N], U8, name="w4_sc", align_bytes=64)
-        nc.gpsimd.memset(w4_sc[:].bitcast(I32), 0)
-        load_packed_rows(nc.gpsimd, w4_sc, w4_scales)
-
-        gain_rows = stage.tile([P, P], F32, name="gain_rows", tag="s5", align_bytes=64)
-        ident = stage.tile([P, P], F32, name="ident", tag="s6", align_bytes=64)
-        nc.gpsimd.memset(gain_rows[:], 0.0)
+        gain_rows = keep.tile([P, P], F32, name="gain_rows")
+        nc.vector.memset(gain_rows[:], 0.0)
         for b in range(PASSES):
-            nc.gpsimd.dma_start(
+            nc.scalar.dma_start(
                 out=gain_rows[PACK * b : PACK * (b + 1), :].rearrange("t (q i) -> t q i", i=8),
                 in_=gain[K_PASS * b : K_PASS * (b + 1)].rearrange("(q t i) -> t q i", t=PACK, i=8),
             )
-        make_identity(nc, ident[:])
-        gain_ps = psum_gain.tile([P, P], F32, name="gain_ps")
+        gain_ps = psum.tile([P, P], F32, name="gain_ps", tag="acc")
         nc.tensor.transpose(gain_ps[:], gain_rows[:], ident[:])
+        gains = keep.tile([P, PASSES * PACK], F32, name="gains")
+        nc.scalar.copy(out=gains[:], in_=gain_ps[:, 0 : PASSES * PACK])
+        w4_sc = keep.tile([P, N], U8, name="w4_sc", align_bytes=64)
+        nc.vector.memset(w4_sc[:].bitcast(I32), 0)
+        load_packed_rows(nc.scalar, w4_sc, w4_scales)
 
-        w2_sc_raw = keep.tile([P, PASSES, R], U8, name="w2_sc_raw", align_bytes=64)
-        nc.gpsimd.memset(w2_sc_raw[:].rearrange("p a n -> p (a n)").bitcast(I32), 0)
-        for q in range(4):
-            nc.gpsimd.dma_start(
-                out=w2_sc_raw[32 * q : 32 * q + 4, :, :].bitcast(I32),
-                in_=w2_scales[:, 4 * q : 4 * q + 4, :].rearrange("a r n -> r a n").bitcast(I32),
-            )
         v_sc_low = keep.tile([P, S], U8, name="v_sc_low", align_bytes=64)
         nc.gpsimd.memset(v_sc_low[:].bitcast(I32), 0)
-        tab2_sc = keep.tile([P, T2], U8, name="tab2_sc", align_bytes=64)
-        nc.gpsimd.memset(tab2_sc[:].bitcast(I32), 0)
-        load_packed_rows(nc.gpsimd, tab2_sc, tab2_scales)
 
         v_w = [keep.tile([P, S], U32, name="v_w0", align_bytes=64)]
         nc.vector.tensor_copy(out=v_w[0][:], in_=tab_w[0][:].indirect(idx[:]))
@@ -122,8 +112,6 @@ def tile_list_cartilage_wear_scores_kernel(
                 nc.sync.dma_start(out=w3_raw[:, b, t, :], in_=rows[t])
         for a in range(PASSES):
             nc.sync.dma_start(out=w5_raw[:, a], in_=w5[K_PASS * a : K_PASS * (a + 1), :].rearrange("(p j) c -> p j c", j=PACK))
-        w2_raw = stage.tile([P, PASSES, 2 * R], U8, name="w2_raw", tag="s5", align_bytes=64)
-        nc.sync.dma_start(out=w2_raw[:].bitcast(I32), in_=w2_words.rearrange("a p n -> p a n").bitcast(I32))
         for q in range(4):
             nc.sync.dma_start(out=v_sc_low[32 * q : 32 * q + 4, :].bitcast(I32), in_=v_sc[32 * q + 4 : 32 * q + 8, :].bitcast(I32))
 
@@ -181,7 +169,7 @@ def tile_list_cartilage_wear_scores_kernel(
             nc.vector.tensor_tensor(
                 out=woven(h_bf[b][:, WIDE * pair : WIDE * (pair + 1)]),
                 in0=woven(values),
-                in1=gain_ps[:, PACK * b : PACK * (b + 1)].unsqueeze(1).to_broadcast([P, PAIR * CHUNK, PACK]),
+                in1=gains[:, PACK * b : PACK * (b + 1)].unsqueeze(1).to_broadcast([P, PAIR * CHUNK, PACK]),
                 op=MULT,
             )
 
@@ -199,9 +187,9 @@ def tile_list_cartilage_wear_scores_kernel(
             codes, scales = w1_q[a]
             return (codes[:, P * t : P * (t + 1)].bitcast(FP8X4), scales[:, P * t : P * (t + 1)])
 
-        jobs = [("cos", pair) for pair in range(4)] + [("sin", pair) for pair in range(4)]
+        jobs = [("cos", 0), ("cos", 1), ("cos", 2), ("sin", 0), ("cos", 3), ("sin", 1), ("sin", 2), ("sin", 3)]
         state = [dict() for job in jobs]
-        holds = {0: "w1_grouped0", 1: "w1_grouped1", 7: "v2_sc"}
+        holds = {0: "w1_grouped0", 9: "w1_grouped1", 7: "v2_sc", 2: "w2_raw", 3: "w2_sc_raw", 4: "tab2_sc"}
 
         def multiply(j):
             kind, pair = jobs[j]
@@ -222,7 +210,7 @@ def tile_list_cartilage_wear_scores_kernel(
             if j in holds:
                 turns = stage.tile([P, WIDE], F32, name="turns%d" % j, tag=holds[j], align_bytes=64)
             else:
-                turns = ring.tile([P, WIDE], F32, name="turns", bufs=3)
+                turns = ring.tile([P, WIDE], F32, name="turns", bufs=2)
             state[j]["turns"] = turns
             for side, bank in enumerate(state[j]["banks"]):
                 dst = turns[:, BANK * side : BANK * (side + 1)]
@@ -258,7 +246,7 @@ def tile_list_cartilage_wear_scores_kernel(
         steps = (multiply, to_turns, round_turns, take_rest, sine, weigh, finish)
         lags = (0, 1, 2, 3, 4, 5, 6)
         for step in range(len(jobs) + lags[-1]):
-            if step in (3, 3 + 1):
+            if step in (2, 2 + 1):
                 w1_q.append(quantize_w1(len(w1_q)))
                 if len(w1_q) == PASSES:
                     tab2_w = stage.tile([P, PASSES, T2], U32, name="tab2_w", tag="s1", align_bytes=64)
@@ -267,19 +255,33 @@ def tile_list_cartilage_wear_scores_kernel(
             for work, lag in zip(steps, lags):
                 if 0 <= step - lag < len(jobs):
                     work(step - lag)
+            if step == 6:
+                w2_raw = stage.tile([P, PASSES, 2 * R], U8, name="w2_raw", tag="w2_raw", align_bytes=64)
+                nc.sync.dma_start(out=w2_raw[:].bitcast(I32), in_=w2_words.rearrange("a p n -> p a n").bitcast(I32))
+                w2_sc_raw = stage.tile([P, PASSES, R], U8, name="w2_sc_raw", tag="w2_sc_raw", align_bytes=64)
+                nc.vector.memset(w2_sc_raw[:].rearrange("p a n -> p (a n)").bitcast(I32), 0)
+                for q in range(4):
+                    nc.sync.dma_start(
+                        out=w2_sc_raw[32 * q : 32 * q + 4, :, :].bitcast(I32),
+                        in_=w2_scales[:, 4 * q : 4 * q + 4, :].rearrange("a r n -> r a n").bitcast(I32),
+                    )
+            if step == 8:
+                tab2_sc = stage.tile([P, T2], U8, name="tab2_sc", tag="tab2_sc", align_bytes=64)
+                nc.vector.memset(tab2_sc[:].bitcast(I32), 0)
+                load_packed_rows(nc.sync, tab2_sc, tab2_scales)
+            if step == 9:
+                w2_w = keep.tile([P, PASSES, 2 * R], U8, name="w2_w", align_bytes=64)
+                nc.vector.tensor_copy(
+                    out=w2_w[:].bitcast(I32).rearrange("p a (t q w) -> p a t q w", t=PACK, w=4),
+                    in_=w2_raw[:].bitcast(I32).rearrange("p a (q t w) -> p a t q w", t=PACK, w=4),
+                )
+                w2_sc = keep.tile([P, PASSES, R], U8, name="w2_sc", align_bytes=64)
+                nc.vector.tensor_copy(
+                    out=w2_sc[:].bitcast(I32).rearrange("p a (t q w) -> p a t q w", t=PACK, w=2),
+                    in_=w2_sc_raw[:].bitcast(I32).rearrange("p a (q t w) -> p a t q w", t=PACK, w=2),
+                )
             if step in (6, 6 + 2):
                 w3_q.append(quantize_weight("w3_%d" % len(w3_q), w3_raw[:, len(w3_q)], "scalar"))
-
-        w2_w = keep.tile([P, PASSES, 2 * R], U8, name="w2_w", align_bytes=64)
-        nc.vector.tensor_copy(
-            out=w2_w[:].bitcast(I32).rearrange("p a (t q w) -> p a t q w", t=PACK, w=4),
-            in_=w2_raw[:].bitcast(I32).rearrange("p a (q t w) -> p a t q w", t=PACK, w=4),
-        )
-        w2_sc = keep.tile([P, PASSES, R], U8, name="w2_sc", align_bytes=64)
-        nc.vector.tensor_copy(
-            out=w2_sc[:].bitcast(I32).rearrange("p a (t q w) -> p a t q w", t=PACK, w=2),
-            in_=w2_sc_raw[:].bitcast(I32).rearrange("p a (q t w) -> p a t q w", t=PACK, w=2),
-        )
 
         def w2_of(a, t):
             return (w2_w[:, a, 2 * P * t : 2 * P * (t + 1)].bitcast(FP4X4), w2_sc[:, a, P * t : P * (t + 1)])
@@ -325,7 +327,7 @@ def tile_list_cartilage_wear_scores_kernel(
                 lambda a: (w5_q[a][0][:, P * n : P * (n + 1)].bitcast(FP8X4), w5_q[a][1][:, P * n : P * (n + 1)]),
                 lambda a: (v2_w[:, a, :].bitcast(FP8X4), v2_sc[4 * a : P, :]),
             )
-            own = ring.tile([P, TRIALS], F32, name="own", bufs=3)
+            own = ring.tile([P, TRIALS], F32, name="own", bufs=4)
             nc.scalar.copy(out=own[:], in_=acc)
             result = ring.tile([P, TRIALS], F32, name="result")
             nc.vector.tensor_tensor(out=result[:], in0=scores[n][:].indirect(picks[:]), in1=own[:], op=ADD)

@@ -24,13 +24,23 @@ P = 128
 PACK = 4
 K_PASS = P * PACK
 PASSES = 2
+QUADS = 4
+ROWS = 4
 BANK = 512
-CHUNK = 128
+CHUNK = BANK // PACK
 PAIR = 2
 WIDE = PAIR * BANK
+PAIRS = S // (PAIR * CHUNK)
 HALVES = S // BANK
 TILES = N // P
+LIST_COLS = BANK // 16
+DEPTH = 3
 TWO_PI = 2.0 * math.pi
+
+JOBS = (("cos", 0), ("cos", 1), ("cos", 2), ("sin", 0), ("cos", 3), ("sin", 1), ("sin", 2), ("sin", 3))
+TURNS_TAG = {0: "w1_grouped0", 1: "w1_grouped1", 2: "w2_raw", 3: "w2_sc_raw", 4: "tab2_sc", 7: "v2_sc"}
+W1_STEPS, W2_LOAD_STEP, W3_STEPS, TAB2_SC_STEP, W2_DEAL_STEP = (2, 3), 6, (6, 8), 8, 9
+W5_STEPS = (0, 2)
 
 
 def tile_list_cartilage_wear_scores_kernel(
@@ -45,18 +55,19 @@ def tile_list_cartilage_wear_scores_kernel(
         ring = ctx.enter_context(tc.tile_pool(name="ring", bufs=2))
         psum = ctx.enter_context(tc.psum_pool(name="psum", bufs=8))
 
-        def load_packed_rows(queue, tile, scales):
-            for q in range(4):
-                queue.dma_start(out=tile[32 * q : 32 * q + 8, :].bitcast(I32), in_=scales[:, 4 * q : 4 * q + 4, :].bitcast(I32))
+        def load_packed_plane(queue, plane, scales):
+            for quad in range(QUADS):
+                queue.dma_start(
+                    out=plane[32 * quad : 32 * quad + PASSES * ROWS, :].bitcast(I32),
+                    in_=scales[:, ROWS * quad : ROWS * (quad + 1), :].bitcast(I32),
+                )
 
-        def cast(engine, dst, src):
-            if engine == "vector":
-                nc.vector.tensor_copy(out=dst, in_=src)
-            elif engine == "scalar":
-                nc.scalar.copy(out=dst, in_=src)
-            else:
-                nc.gpsimd.tensor_scalar(out=dst, in0=src, scalar1=1.0, scalar2=0.0, op0=MULT, op1=ADD)
+        def load_table_pass(a):
+            words = stage.tile([P, T], U32, name="tab_w%d" % a, tag="big%d" % a, align_bytes=64)
+            nc.sync.dma_start(out=words[:].bitcast(I32), in_=tab_words[a].rearrange("p t i -> p (t i)").bitcast(I32))
+            return words
 
+        tab_w = [load_table_pass(0)]
         idx = lists.tile([P, S // 16], U16, name="idx")
         idx2 = lists.tile([P, TRIALS // 16], U16, name="idx2")
         picks = lists.tile([P, TRIALS // 16], U16, name="picks")
@@ -64,18 +75,15 @@ def tile_list_cartilage_wear_scores_kernel(
         nc.sync.dma_start(idx2[:], offs2)
         nc.sync.dma_start(picks[:], pos1)
 
-        ident = keep.tile([P, P], F32, name="ident")
-        make_identity(nc, ident[:])
-        tab_sc = stage.tile([P, T], U8, name="tab_sc", tag="s0", align_bytes=64)
+        tab_sc = stage.tile([P, T], U8, name="tab_sc", tag="tab_sc", align_bytes=64)
         nc.vector.memset(tab_sc[:].bitcast(I32), 0)
-        load_packed_rows(nc.gpsimd, tab_sc, tab_scales)
-        tab_w = []
-        for a in range(PASSES):
-            tile = stage.tile([P, T], U32, name="tab_w%d" % a, tag="s%d" % (1 + a), align_bytes=64)
-            nc.sync.dma_start(out=tile[:].bitcast(I32), in_=tab_words[a].rearrange("p t i -> p (t i)").bitcast(I32))
-            tab_w.append(tile)
+        load_packed_plane(nc.gpsimd, tab_sc, tab_scales)
+        tab_w.append(load_table_pass(1))
         w4_w = keep.tile([P, PASSES, N], U32, name="w4_w", align_bytes=64)
         nc.sync.dma_start(out=w4_w[:].bitcast(I32), in_=w4_words.rearrange("a p c i -> p a (c i)").bitcast(I32))
+
+        ident = keep.tile([P, P], F32, name="ident")
+        make_identity(nc, ident[:])
         gain_rows = keep.tile([P, P], F32, name="gain_rows")
         nc.vector.memset(gain_rows[:], 0.0)
         for b in range(PASSES):
@@ -89,56 +97,63 @@ def tile_list_cartilage_wear_scores_kernel(
         nc.scalar.copy(out=gains[:], in_=gain_ps[:, 0 : PASSES * PACK])
         w4_sc = keep.tile([P, N], U8, name="w4_sc", align_bytes=64)
         nc.vector.memset(w4_sc[:].bitcast(I32), 0)
-        load_packed_rows(nc.scalar, w4_sc, w4_scales)
+        load_packed_plane(nc.scalar, w4_sc, w4_scales)
 
-        v_sc_low = keep.tile([P, S], U8, name="v_sc_low", align_bytes=64)
-        nc.gpsimd.memset(v_sc_low[:].bitcast(I32), 0)
+        v_sc_pass1 = keep.tile([P, S], U8, name="v_sc_pass1", align_bytes=64)
+        nc.vector.memset(v_sc_pass1[:].bitcast(I32), 0)
 
         v_w = [keep.tile([P, S], U32, name="v_w0", align_bytes=64)]
         nc.vector.tensor_copy(out=v_w[0][:], in_=tab_w[0][:].indirect(idx[:]))
         v_sc = keep.tile([P, S], U8, name="v_sc", align_bytes=64)
         nc.vector.tensor_copy(out=v_sc[:], in_=tab_sc[:].indirect(idx[:]))
-        v_w.append(stage.tile([P, S], U32, name="v_w1", tag="s0", align_bytes=64))
+        v_w.append(stage.tile([P, S], U32, name="v_w1", tag="tab_sc", align_bytes=64))
         for half in range(HALVES):
-            nc.vector.tensor_copy(out=v_w[1][:, BANK * half : BANK * (half + 1)], in_=tab_w[1][:].indirect(idx[:, 32 * half : 32 * (half + 1)]))
-        w1_raw = stage.tile([P, PASSES, PACK, R], F32, name="w1_raw", tag="s1", align_bytes=64)
+            nc.vector.tensor_copy(
+                out=v_w[1][:, BANK * half : BANK * (half + 1)],
+                in_=tab_w[1][:].indirect(idx[:, LIST_COLS * half : LIST_COLS * (half + 1)]),
+            )
+
+        w1_raw = stage.tile([P, PASSES, PACK, R], F32, name="w1_raw", tag="big0", align_bytes=64)
         for a in range(PASSES):
             nc.sync.dma_start(out=w1_raw[:, a], in_=w1[K_PASS * a : K_PASS * (a + 1), :].rearrange("(p j) c -> p j c", j=PACK))
-        late_raw = stage.tile([P, 2, PASSES, PACK, N], F32, name="late_raw", tag="s2", align_bytes=64)
-        w3_raw, w5_raw = late_raw[:, 0], late_raw[:, 1]
+        w35_raw = stage.tile([P, 2, PASSES, PACK, N], F32, name="w35_raw", tag="big1", align_bytes=64)
+        w3_raw, w5_raw = w35_raw[:, 0], w35_raw[:, 1]
         for b in range(PASSES):
             rows = w3[K_PASS * b : K_PASS * (b + 1), :].rearrange("(q t i) n -> t q i n", t=PACK, i=8)
             for t in range(PACK):
                 nc.sync.dma_start(out=w3_raw[:, b, t, :], in_=rows[t])
         for a in range(PASSES):
             nc.sync.dma_start(out=w5_raw[:, a], in_=w5[K_PASS * a : K_PASS * (a + 1), :].rearrange("(p j) c -> p j c", j=PACK))
-        for q in range(4):
-            nc.sync.dma_start(out=v_sc_low[32 * q : 32 * q + 4, :].bitcast(I32), in_=v_sc[32 * q + 4 : 32 * q + 8, :].bitcast(I32))
+        for quad in range(QUADS):
+            nc.sync.dma_start(
+                out=v_sc_pass1[32 * quad : 32 * quad + ROWS, :].bitcast(I32),
+                in_=v_sc[32 * quad + ROWS : 32 * quad + 2 * ROWS, :].bitcast(I32),
+            )
 
-        def quantize(name, grouped):
+        def quantize_weight(name, grouped):
             codes = keep.tile([P, N], U32, name=name + "_w", align_bytes=64)
             scales = keep.tile([P, N], U8, name=name + "_sc", align_bytes=64)
             nc.vector.quantize_mx(out=codes[:].bitcast(FP8X4), scales=scales[:], in_=grouped[:])
             return codes, scales
 
-        def quantize_weight(name, raw, engine):
+        def round_on_scalar(name, raw):
             grouped = ring.tile([P, PACK * N], BF16, name="grouped", align_bytes=64)
             width = N // 2
             for lo in range(0, N, width):
-                cast(engine, grouped[:, PACK * lo : PACK * (lo + width)].rearrange("p (c i j) -> p c j i", i=4, j=PACK),
-                     raw[:, :, lo : lo + width].rearrange("p j (c i) -> p c j i", i=4))
-            return quantize(name, grouped)
+                nc.scalar.copy(
+                    out=grouped[:, PACK * lo : PACK * (lo + width)].rearrange("p (c i j) -> p c j i", i=4, j=PACK),
+                    in_=raw[:, :, lo : lo + width].rearrange("p j (c i) -> p c j i", i=4),
+                )
+            return quantize_weight(name, grouped)
 
-        def quantize_w1(a):
+        def round_w1(a):
             grouped = stage.tile([P, PACK * R], BF16, name="w1_grouped%d" % a, tag="w1_grouped%d" % a, align_bytes=64)
-            cast("vector",
-                 grouped[:].rearrange("p (t q i j) -> p t q i j", t=PACK, i=8, j=PACK),
-                 w1_raw[:, a].rearrange("p j (q t i) -> p t q i j", t=PACK, i=8))
-            return quantize("w1_%d" % a, grouped)
-
-        h_bf = [keep.tile([P, S * PACK], BF16, name="h_bf%d" % b, align_bytes=64) for b in range(PASSES)]
-        h_w = [keep.tile([P, S], U32, name="h_w%d" % b, align_bytes=64) for b in range(PASSES)]
-        h_sc = [keep.tile([P, S], U8, name="h_sc%d" % b, align_bytes=64) for b in range(PASSES)]
+            for g in range(2):
+                nc.vector.tensor_copy(
+                    out=grouped[:].rearrange("p (t q g e j) -> p g q t j e", t=PACK, g=2, e=4, j=PACK)[:, g],
+                    in_=w1_raw[:, a].rearrange("p j (q t g e) -> p g q t j e", t=PACK, g=2, e=4)[:, g],
+                )
+            return quantize_weight("w1_%d" % a, grouped)
 
         def woven(ap):
             return ap.rearrange("p (n t) -> p n t", t=PACK)
@@ -165,6 +180,17 @@ def tile_list_cartilage_wear_scores_kernel(
                                     start=(a == 0), stop=(a == PASSES - 1))
             return acc[:]
 
+        def columns(weight, tile):
+            codes, scales = weight
+            return codes[:, P * tile : P * (tile + 1)].bitcast(FP8X4), scales[:, P * tile : P * (tile + 1)]
+
+        def packed_v_sc(a, cols):
+            return v_sc[ROWS * a : P, cols]
+
+        h_bf = [keep.tile([P, S * PACK], BF16, name="h_bf%d" % b, align_bytes=64) for b in range(PASSES)]
+        h_w = [keep.tile([P, S], U32, name="h_w%d" % b, align_bytes=64) for b in range(PASSES)]
+        h_sc = [keep.tile([P, S], U8, name="h_sc%d" % b, align_bytes=64) for b in range(PASSES)]
+
         def scale_by_gain(b, pair, values):
             nc.vector.tensor_tensor(
                 out=woven(h_bf[b][:, WIDE * pair : WIDE * (pair + 1)]),
@@ -179,97 +205,91 @@ def tile_list_cartilage_wear_scores_kernel(
                                   in_=h_bf[b][:, WIDE * pair : WIDE * (pair + 1)])
 
         cosines = keep.tile([P, HALVES * TILES * BANK], F32, name="cosines")
-        rests = stage.tile([P, 3, WIDE], F32, name="rests", tag="s7", align_bytes=64)
-        wholes = stage.tile([P, 3, WIDE], I32, name="wholes", tag="s8", align_bytes=64)
+        rests = stage.tile([P, DEPTH, WIDE], F32, name="rests", tag="rests", align_bytes=64)
+        wholes = stage.tile([P, DEPTH, WIDE], I32, name="wholes", tag="wholes", align_bytes=64)
         w1_q, w3_q, w5_q = [], [], []
-
-        def w1_of(a, t):
-            codes, scales = w1_q[a]
-            return (codes[:, P * t : P * (t + 1)].bitcast(FP8X4), scales[:, P * t : P * (t + 1)])
-
-        jobs = [("cos", 0), ("cos", 1), ("cos", 2), ("sin", 0), ("cos", 3), ("sin", 1), ("sin", 2), ("sin", 3)]
-        state = [dict() for job in jobs]
-        holds = {0: "w1_grouped0", 9: "w1_grouped1", 7: "v2_sc", 2: "w2_raw", 3: "w2_sc_raw", 4: "tab2_sc"}
+        banks, turns, sines = {}, {}, {}
 
         def multiply(j):
-            kind, pair = jobs[j]
-            banks = []
+            kind, pair = JOBS[j]
+            banks[j] = []
             for bank in range(PAIR * pair, PAIR * (pair + 1)):
                 if kind == "cos":
                     half, n = divmod(bank, TILES)
                     cols = slice(BANK * half, BANK * (half + 1))
-                    banks.append(product(
-                        lambda a: (w4_w[:, a, P * n : P * (n + 1)].bitcast(FP8X4), w4_sc[4 * a : P, P * n : P * (n + 1)]),
-                        lambda a: (v_w[a][:, cols].bitcast(FP8X4), v_sc[4 * a : P, cols]),
+                    banks[j].append(product(
+                        lambda a: (w4_w[:, a, P * n : P * (n + 1)].bitcast(FP8X4), w4_sc[ROWS * a : P, P * n : P * (n + 1)]),
+                        lambda a: (v_w[a][:, cols].bitcast(FP8X4), packed_v_sc(a, cols)),
                     ))
                 else:
-                    banks.append(feature_bank(bank, w1_of, lambda a, cols: v_sc[4 * a : P, cols]))
-            state[j]["banks"] = banks
+                    banks[j].append(feature_bank(bank, lambda a, t: columns(w1_q[a], t), packed_v_sc))
 
         def to_turns(j):
-            if j in holds:
-                turns = stage.tile([P, WIDE], F32, name="turns%d" % j, tag=holds[j], align_bytes=64)
+            if j in TURNS_TAG:
+                turns[j] = stage.tile([P, WIDE], F32, name="turns%d" % j, tag=TURNS_TAG[j], align_bytes=64)
             else:
-                turns = ring.tile([P, WIDE], F32, name="turns", bufs=2)
-            state[j]["turns"] = turns
-            for side, bank in enumerate(state[j]["banks"]):
-                dst = turns[:, BANK * side : BANK * (side + 1)]
-                if jobs[j][0] == "cos":
+                turns[j] = ring.tile([P, WIDE], F32, name="turns")
+            for side, bank in enumerate(banks[j]):
+                dst = turns[j][:, BANK * side : BANK * (side + 1)]
+                if JOBS[j][0] == "cos":
                     nc.scalar.activation(out=dst, in_=bank, func=ACT.Copy, scale=1.0 / TWO_PI, bias=0.25)
                 else:
                     nc.scalar.activation(out=woven(dst), in_=bank, func=ACT.Copy, scale=1.0 / TWO_PI)
 
         def round_turns(j):
-            nc.vector.tensor_copy(out=wholes[:, j % 3], in_=state[j]["turns"][:])
+            width = BANK if j == 0 else WIDE
+            for lo in range(0, WIDE, width):
+                nc.vector.tensor_copy(out=wholes[:, j % DEPTH, lo : lo + width], in_=turns[j][:, lo : lo + width])
 
         def take_rest(j):
-            nc.vector.tensor_tensor(out=rests[:, j % 3], in0=state[j]["turns"][:], in1=wholes[:, j % 3], op=SUB)
+            width = BANK if j == 0 else WIDE
+            for lo in range(0, WIDE, width):
+                cols = slice(lo, lo + width)
+                nc.vector.tensor_tensor(out=rests[:, j % DEPTH, cols], in0=turns[j][:, cols], in1=wholes[:, j % DEPTH, cols], op=SUB)
 
         def sine(j):
-            kind, pair = jobs[j]
+            kind, pair = JOBS[j]
             if kind == "cos":
                 dst = cosines[:, WIDE * pair : WIDE * (pair + 1)]
             else:
-                values = ring.tile([P, WIDE], F32, name="values", bufs=2)
-                dst = values[:]
-                state[j]["values"] = dst
-            nc.scalar.activation(out=dst, in_=rests[:, j % 3], func=ACT.Sin, scale=TWO_PI)
+                sines[j] = ring.tile([P, WIDE], F32, name="sines")
+                dst = sines[j][:]
+            nc.scalar.activation(out=dst, in_=rests[:, j % DEPTH], func=ACT.Sin, scale=TWO_PI)
 
         def weigh(j):
-            if jobs[j][0] == "sin":
-                scale_by_gain(0, jobs[j][1], state[j]["values"])
+            if j in sines:
+                scale_by_gain(0, JOBS[j][1], sines[j][:])
 
         def finish(j):
-            if jobs[j][0] == "sin":
-                quantize_h(0, jobs[j][1])
+            if j in sines:
+                quantize_h(0, JOBS[j][1])
 
-        steps = (multiply, to_turns, round_turns, take_rest, sine, weigh, finish)
-        lags = (0, 1, 2, 3, 4, 5, 6)
-        for step in range(len(jobs) + lags[-1]):
-            if step in (2, 2 + 1):
-                w1_q.append(quantize_w1(len(w1_q)))
-                if len(w1_q) == PASSES:
-                    tab2_w = stage.tile([P, PASSES, T2], U32, name="tab2_w", tag="s1", align_bytes=64)
-                    for a in range(PASSES):
-                        nc.sync.dma_start(out=tab2_w[:, a, :].bitcast(I32), in_=tab2_words[a].rearrange("p t i -> p (t i)").bitcast(I32))
-            for work, lag in zip(steps, lags):
-                if 0 <= step - lag < len(jobs):
+        stages = (multiply, to_turns, round_turns, take_rest, sine, weigh, finish)
+        for step in range(len(JOBS) + len(stages) - 1):
+            if step in W1_STEPS:
+                w1_q.append(round_w1(len(w1_q)))
+            if step == W1_STEPS[-1]:
+                tab2_w = stage.tile([P, PASSES, T2], U32, name="tab2_w", tag="big0", align_bytes=64)
+                for a in range(PASSES):
+                    nc.sync.dma_start(out=tab2_w[:, a, :].bitcast(I32), in_=tab2_words[a].rearrange("p t i -> p (t i)").bitcast(I32))
+            for lag, work in enumerate(stages):
+                if 0 <= step - lag < len(JOBS):
                     work(step - lag)
-            if step == 6:
+            if step == W2_LOAD_STEP:
                 w2_raw = stage.tile([P, PASSES, 2 * R], U8, name="w2_raw", tag="w2_raw", align_bytes=64)
                 nc.sync.dma_start(out=w2_raw[:].bitcast(I32), in_=w2_words.rearrange("a p n -> p a n").bitcast(I32))
                 w2_sc_raw = stage.tile([P, PASSES, R], U8, name="w2_sc_raw", tag="w2_sc_raw", align_bytes=64)
                 nc.vector.memset(w2_sc_raw[:].rearrange("p a n -> p (a n)").bitcast(I32), 0)
-                for q in range(4):
+                for quad in range(QUADS):
                     nc.sync.dma_start(
-                        out=w2_sc_raw[32 * q : 32 * q + 4, :, :].bitcast(I32),
-                        in_=w2_scales[:, 4 * q : 4 * q + 4, :].rearrange("a r n -> r a n").bitcast(I32),
+                        out=w2_sc_raw[32 * quad : 32 * quad + ROWS, :, :].bitcast(I32),
+                        in_=w2_scales[:, ROWS * quad : ROWS * (quad + 1), :].rearrange("a r n -> r a n").bitcast(I32),
                     )
-            if step == 8:
+            if step == TAB2_SC_STEP:
                 tab2_sc = stage.tile([P, T2], U8, name="tab2_sc", tag="tab2_sc", align_bytes=64)
                 nc.vector.memset(tab2_sc[:].bitcast(I32), 0)
-                load_packed_rows(nc.sync, tab2_sc, tab2_scales)
-            if step == 9:
+                load_packed_plane(nc.sync, tab2_sc, tab2_scales)
+            if step == W2_DEAL_STEP:
                 w2_w = keep.tile([P, PASSES, 2 * R], U8, name="w2_w", align_bytes=64)
                 nc.vector.tensor_copy(
                     out=w2_w[:].bitcast(I32).rearrange("p a (t q w) -> p a t q w", t=PACK, w=4),
@@ -280,55 +300,48 @@ def tile_list_cartilage_wear_scores_kernel(
                     out=w2_sc[:].bitcast(I32).rearrange("p a (t q w) -> p a t q w", t=PACK, w=2),
                     in_=w2_sc_raw[:].bitcast(I32).rearrange("p a (q t w) -> p a t q w", t=PACK, w=2),
                 )
-            if step in (6, 6 + 2):
-                w3_q.append(quantize_weight("w3_%d" % len(w3_q), w3_raw[:, len(w3_q)], "scalar"))
-
-        def w2_of(a, t):
-            return (w2_w[:, a, 2 * P * t : 2 * P * (t + 1)].bitcast(FP4X4), w2_sc[:, a, P * t : P * (t + 1)])
+            if step in W3_STEPS:
+                w3_q.append(round_on_scalar("w3_%d" % len(w3_q), w3_raw[:, len(w3_q)]))
 
         v2_sc = stage.tile([P, TRIALS], U8, name="v2_sc", tag="v2_sc", align_bytes=64)
         nc.vector.tensor_copy(out=v2_sc[:], in_=tab2_sc[:].indirect(idx2[:]))
-        v2_w = stage.tile([P, PASSES, TRIALS], U32, name="v2_w", tag="s8", align_bytes=64)
+        v2_w = stage.tile([P, PASSES, TRIALS], U32, name="v2_w", tag="wholes", align_bytes=64)
         for a in range(PASSES):
             nc.vector.tensor_copy(out=v2_w[:, a, :], in_=tab2_w[:, a, :].indirect(idx2[:]))
 
-        exps = stage.tile([P, 3, WIDE], F32, name="exps", tag="s7", align_bytes=64)
-        pairs = S // (PAIR * CHUNK)
-        for step in range(pairs + 2):
-            if step < pairs:
+        def w2_columns(a, t):
+            return w2_w[:, a, 2 * P * t : 2 * P * (t + 1)].bitcast(FP4X4), w2_sc[:, a, P * t : P * (t + 1)]
+
+        exps = stage.tile([P, DEPTH, WIDE], F32, name="exps", tag="rests", align_bytes=64)
+        for step in range(PAIRS + 2):
+            if step < PAIRS:
                 for side in range(PAIR):
-                    bank = feature_bank(PAIR * step + side, w2_of, lambda a, cols: (v_sc, v_sc_low)[a][:, cols])
-                    nc.scalar.activation(out=woven(exps[:, step % 3, BANK * side : BANK * (side + 1)]), in_=bank, func=ACT.Exp)
-            if 0 <= step - 1 < pairs:
-                scale_by_gain(1, step - 1, exps[:, (step - 1) % 3])
-            if 0 <= step - 2 < pairs:
+                    bank = feature_bank(PAIR * step + side, w2_columns, lambda a, cols: (v_sc, v_sc_pass1)[a][:, cols])
+                    nc.scalar.activation(out=woven(exps[:, step % DEPTH, BANK * side : BANK * (side + 1)]), in_=bank, func=ACT.Exp)
+            if 0 <= step - 1 < PAIRS:
+                scale_by_gain(1, step - 1, exps[:, (step - 1) % DEPTH])
+            if 0 <= step - 2 < PAIRS:
                 quantize_h(1, step - 2)
-            if step in (0, 0 + 2):
-                w5_q.append(quantize_weight("w5_%d" % len(w5_q), w5_raw[:, len(w5_q)], "scalar"))
+            if step in W5_STEPS:
+                w5_q.append(round_on_scalar("w5_%d" % len(w5_q), w5_raw[:, len(w5_q)]))
 
         scores = [keep.tile([P, S], F32, name="y%d" % n) for n in range(TILES)]
 
         def second_stage(n, half):
             cols = slice(BANK * half, BANK * (half + 1))
-            acc = product(
-                lambda b: (w3_q[b][0][:, P * n : P * (n + 1)].bitcast(FP8X4), w3_q[b][1][:, P * n : P * (n + 1)]),
-                lambda b: (h_w[b][:, cols].bitcast(FP8X4), h_sc[b][:, cols]),
-            )
-            d = ring.tile([P, BANK], F32, name="d", bufs=3)
-            nc.scalar.activation(out=d[:], in_=acc, func=ACT.Tanh)
+            acc = product(lambda b: columns(w3_q[b], n), lambda b: (h_w[b][:, cols].bitcast(FP8X4), h_sc[b][:, cols]))
+            squashed = ring.tile([P, BANK], F32, name="squashed", bufs=DEPTH)
+            nc.scalar.activation(out=squashed[:], in_=acc, func=ACT.Tanh)
             bank = TILES * half + n
-            nc.vector.tensor_tensor(out=scores[n][:, cols], in0=d[:], in1=cosines[:, BANK * bank : BANK * (bank + 1)], op=MULT)
+            nc.vector.tensor_tensor(out=scores[n][:, cols], in0=squashed[:], in1=cosines[:, BANK * bank : BANK * (bank + 1)], op=MULT)
 
         for n in range(TILES):
             second_stage(n, 0)
         for n in range(TILES):
             second_stage(n, 1)
-            acc = product(
-                lambda a: (w5_q[a][0][:, P * n : P * (n + 1)].bitcast(FP8X4), w5_q[a][1][:, P * n : P * (n + 1)]),
-                lambda a: (v2_w[:, a, :].bitcast(FP8X4), v2_sc[4 * a : P, :]),
-            )
-            own = ring.tile([P, TRIALS], F32, name="own", bufs=4)
+            acc = product(lambda a: columns(w5_q[a], n), lambda a: (v2_w[:, a, :].bitcast(FP8X4), v2_sc[ROWS * a : P, :]))
+            own = ring.tile([P, TRIALS], F32, name="own", bufs=DEPTH)
             nc.scalar.copy(out=own[:], in_=acc)
-            result = ring.tile([P, TRIALS], F32, name="result")
+            result = ring.tile([P, TRIALS], F32, name="result", bufs=DEPTH)
             nc.vector.tensor_tensor(out=result[:], in0=scores[n][:].indirect(picks[:]), in1=own[:], op=ADD)
             nc.sync.dma_start(out=out[P * n : P * (n + 1), :], in_=result[:])

import math
from contextlib import ExitStack

import concourse.mybir as mybir
from concourse.masks import make_identity

K, T, S, T2, TRIALS, R, H, N = 1024, 4096, 1024, 2048, 512, 512, 1024, 512
FLOPS = 2 * K * S * (R + (H - R) + N) + 2 * H * N * S + 2 * K * N * TRIALS

F32 = mybir.dt.float32
BF16 = mybir.dt.bfloat16
I32 = mybir.dt.int32
U32 = mybir.dt.uint32
U16 = mybir.dt.uint16
U8 = mybir.dt.uint8
FP8X4 = mybir.dt.float8_e4m3fn_x4
FP4X4 = mybir.dt.float4_e2m1fn_x4
ACT = mybir.ActivationFunctionType
MULT = mybir.AluOpType.mult
ADD = mybir.AluOpType.add
SUB = mybir.AluOpType.subtract

P = 128
PACK = 4
K_PASS = P * PACK
PASSES = 2
QUADS = 4
ROWS = 4
BANK = 512
CHUNK = BANK // PACK
PAIR = 2
WIDE = PAIR * BANK
PAIRS = S // (PAIR * CHUNK)
HALVES = S // BANK
TILES = N // P
LIST_COLS = BANK // 16
DEPTH = 3
TWO_PI = 2.0 * math.pi

JOBS = (("cos", 0), ("cos", 1), ("cos", 2), ("sin", 0), ("cos", 3), ("sin", 1), ("sin", 2), ("sin", 3))
TURNS_TAG = {0: "w1_grouped0", 1: "w1_grouped1", 2: "w2_raw", 3: "w2_sc_raw", 4: "tab2_sc", 7: "v2_sc"}
W1_STEPS, W2_LOAD_STEP, W3_STEPS, TAB2_SC_STEP, W2_DEAL_STEP = (2, 3), 6, (6, 8), 8, 9
W5_STEPS = (0, 2)


def tile_list_cartilage_wear_scores_kernel(
    tc, tab_words, tab_scales, tab2_words, tab2_scales, offs, offs2, pos1,
    w1, w2_words, w2_scales, gain, w3, w4_words, w4_scales, w5, out,
):
    nc = tc.nc
    with ExitStack() as ctx:
        lists = ctx.enter_context(tc.tile_pool(name="lists", bufs=1))
        keep = ctx.enter_context(tc.tile_pool(name="keep", bufs=1))
        stage = ctx.enter_context(tc.tile_pool(name="stage", bufs=1))
        ring = ctx.enter_context(tc.tile_pool(name="ring", bufs=2))
        psum = ctx.enter_context(tc.psum_pool(name="psum", bufs=8))

        def load_packed_plane(queue, plane, scales):
            for quad in range(QUADS):
                queue.dma_start(
                    out=plane[32 * quad : 32 * quad + PASSES * ROWS, :].bitcast(I32),
                    in_=scales[:, ROWS * quad : ROWS * (quad + 1), :].bitcast(I32),
                )

        def load_table_pass(a):
            words = stage.tile([P, T], U32, name="tab_w%d" % a, tag="big%d" % a, align_bytes=64)
            nc.sync.dma_start(out=words[:].bitcast(I32), in_=tab_words[a].rearrange("p t i -> p (t i)").bitcast(I32))
            return words

        tab_w = [load_table_pass(0)]
        idx = lists.tile([P, S // 16], U16, name="idx")
        idx2 = lists.tile([P, TRIALS // 16], U16, name="idx2")
        picks = lists.tile([P, TRIALS // 16], U16, name="picks")
        nc.sync.dma_start(idx[:], offs)
        nc.sync.dma_start(idx2[:], offs2)
        nc.sync.dma_start(picks[:], pos1)

        tab_sc = stage.tile([P, T], U8, name="tab_sc", tag="tab_sc", align_bytes=64)
        nc.vector.memset(tab_sc[:].bitcast(I32), 0)
        load_packed_plane(nc.gpsimd, tab_sc, tab_scales)
        tab_w.append(load_table_pass(1))
        w4_w = keep.tile([P, PASSES, N], U32, name="w4_w", align_bytes=64)
        nc.sync.dma_start(out=w4_w[:].bitcast(I32), in_=w4_words.rearrange("a p c i -> p a (c i)").bitcast(I32))

        ident = keep.tile([P, P], F32, name="ident")
        make_identity(nc, ident[:])
        gain_rows = keep.tile([P, P], F32, name="gain_rows")
        nc.vector.memset(gain_rows[:], 0.0)
        for b in range(PASSES):
            nc.scalar.dma_start(
                out=gain_rows[PACK * b : PACK * (b + 1), :].rearrange("t (q i) -> t q i", i=8),
                in_=gain[K_PASS * b : K_PASS * (b + 1)].rearrange("(q t i) -> t q i", t=PACK, i=8),
            )
        gain_ps = psum.tile([P, P], F32, name="gain_ps", tag="acc")
        nc.tensor.transpose(gain_ps[:], gain_rows[:], ident[:])
        gains = keep.tile([P, PASSES * PACK], F32, name="gains")
        nc.scalar.copy(out=gains[:], in_=gain_ps[:, 0 : PASSES * PACK])
        w4_sc = keep.tile([P, N], U8, name="w4_sc", align_bytes=64)
        nc.vector.memset(w4_sc[:].bitcast(I32), 0)
        load_packed_plane(nc.scalar, w4_sc, w4_scales)

        v_sc_pass1 = keep.tile([P, S], U8, name="v_sc_pass1", align_bytes=64)
        nc.vector.memset(v_sc_pass1[:].bitcast(I32), 0)

        v_w = [keep.tile([P, S], U32, name="v_w0", align_bytes=64)]
        nc.vector.tensor_copy(out=v_w[0][:], in_=tab_w[0][:].indirect(idx[:]))
        v_sc = keep.tile([P, S], U8, name="v_sc", align_bytes=64)
        nc.vector.tensor_copy(out=v_sc[:], in_=tab_sc[:].indirect(idx[:]))
        v_w.append(stage.tile([P, S], U32, name="v_w1", tag="tab_sc", align_bytes=64))
        for half in range(HALVES):
            nc.vector.tensor_copy(
                out=v_w[1][:, BANK * half : BANK * (half + 1)],
                in_=tab_w[1][:].indirect(idx[:, LIST_COLS * half : LIST_COLS * (half + 1)]),
            )

        w1_raw = stage.tile([P, PASSES, PACK, R], F32, name="w1_raw", tag="big0", align_bytes=64)
        for a in range(PASSES):
            nc.sync.dma_start(out=w1_raw[:, a], in_=w1[K_PASS * a : K_PASS * (a + 1), :].rearrange("(p j) c -> p j c", j=PACK))
        w35_raw = stage.tile([P, 2, PASSES, PACK, N], F32, name="w35_raw", tag="big1", align_bytes=64)
        w3_raw, w5_raw = w35_raw[:, 0], w35_raw[:, 1]
        for b in range(PASSES):
            rows = w3[K_PASS * b : K_PASS * (b + 1), :].rearrange("(q t i) n -> t q i n", t=PACK, i=8)
            for t in range(PACK):
                nc.sync.dma_start(out=w3_raw[:, b, t, :], in_=rows[t])
        for a in range(PASSES):
            nc.sync.dma_start(out=w5_raw[:, a], in_=w5[K_PASS * a : K_PASS * (a + 1), :].rearrange("(p j) c -> p j c", j=PACK))
        for quad in range(QUADS):
            nc.sync.dma_start(
                out=v_sc_pass1[32 * quad : 32 * quad + ROWS, :].bitcast(I32),
                in_=v_sc[32 * quad + ROWS : 32 * quad + 2 * ROWS, :].bitcast(I32),
            )

        def quantize_weight(name, grouped):
            codes = keep.tile([P, N], U32, name=name + "_w", align_bytes=64)
            scales = keep.tile([P, N], U8, name=name + "_sc", align_bytes=64)
            nc.vector.quantize_mx(out=codes[:].bitcast(FP8X4), scales=scales[:], in_=grouped[:])
            return codes, scales

        def round_on_scalar(name, raw):
            grouped = ring.tile([P, PACK * N], BF16, name="grouped", align_bytes=64)
            width = N // 2
            for lo in range(0, N, width):
                nc.scalar.copy(
                    out=grouped[:, PACK * lo : PACK * (lo + width)].rearrange("p (c i j) -> p c j i", i=4, j=PACK),
                    in_=raw[:, :, lo : lo + width].rearrange("p j (c i) -> p c j i", i=4),
                )
            return quantize_weight(name, grouped)

        def round_w1(a):
            grouped = stage.tile([P, PACK * R], BF16, name="w1_grouped%d" % a, tag="w1_grouped%d" % a, align_bytes=64)
            for g in range(2):
                nc.vector.tensor_copy(
                    out=grouped[:].rearrange("p (t q g e j) -> p g q t j e", t=PACK, g=2, e=4, j=PACK)[:, g],
                    in_=w1_raw[:, a].rearrange("p j (q t g e) -> p g q t j e", t=PACK, g=2, e=4)[:, g],
                )
            return quantize_weight("w1_%d" % a, grouped)

        def woven(ap):
            return ap.rearrange("p (n t) -> p n t", t=PACK)

        def feature_bank(chunk, lhs_of, plane_of):
            cols = slice(chunk * CHUNK, (chunk + 1) * CHUNK)
            acc = psum.tile([P, PACK, CHUNK], F32, name="acc", tag="acc")
            for t in range(PACK):
                for a in range(PASSES):
                    lhs, lhs_sc = lhs_of(a, t)
                    nc.tensor.matmul_mx(
                        out=acc[:, t, :], lhsT=lhs, lhsT_scale=lhs_sc,
                        rhs=v_w[a][:, cols].bitcast(FP8X4), rhs_scale=plane_of(a, cols),
                        start=(a == 0), stop=(a == PASSES - 1),
                    )
            return acc[:].rearrange("p t n -> p n t")

        def product(lhs_of, rhs_of):
            acc = psum.tile([P, BANK], F32, name="acc", tag="acc")
            for a in range(PASSES):
                lhs, lhs_sc = lhs_of(a)
                rhs, rhs_sc = rhs_of(a)
                nc.tensor.matmul_mx(out=acc[:], lhsT=lhs, lhsT_scale=lhs_sc, rhs=rhs, rhs_scale=rhs_sc,
                                    start=(a == 0), stop=(a == PASSES - 1))
            return acc[:]

        def columns(weight, tile):
            codes, scales = weight
            return codes[:, P * tile : P * (tile + 1)].bitcast(FP8X4), scales[:, P * tile : P * (tile + 1)]

        def packed_v_sc(a, cols):
            return v_sc[ROWS * a : P, cols]

        h_bf = [keep.tile([P, S * PACK], BF16, name="h_bf%d" % b, align_bytes=64) for b in range(PASSES)]
        h_w = [keep.tile([P, S], U32, name="h_w%d" % b, align_bytes=64) for b in range(PASSES)]
        h_sc = [keep.tile([P, S], U8, name="h_sc%d" % b, align_bytes=64) for b in range(PASSES)]

        def scale_by_gain(b, pair, values):
            nc.vector.tensor_tensor(
                out=woven(h_bf[b][:, WIDE * pair : WIDE * (pair + 1)]),
                in0=woven(values),
                in1=gains[:, PACK * b : PACK * (b + 1)].unsqueeze(1).to_broadcast([P, PAIR * CHUNK, PACK]),
                op=MULT,
            )

        def quantize_h(b, pair):
            cols = slice(PAIR * CHUNK * pair, PAIR * CHUNK * (pair + 1))
            nc.vector.quantize_mx(out=h_w[b][:, cols].bitcast(FP8X4), scales=h_sc[b][:, cols],
                                  in_=h_bf[b][:, WIDE * pair : WIDE * (pair + 1)])

        cosines = keep.tile([P, HALVES * TILES * BANK], F32, name="cosines")
        rests = stage.tile([P, DEPTH, WIDE], F32, name="rests", tag="rests", align_bytes=64)
        wholes = stage.tile([P, DEPTH, WIDE], I32, name="wholes", tag="wholes", align_bytes=64)
        w1_q, w3_q, w5_q = [], [], []
        banks, turns, sines = {}, {}, {}

        def multiply(j):
            kind, pair = JOBS[j]
            banks[j] = []
            for bank in range(PAIR * pair, PAIR * (pair + 1)):
                if kind == "cos":
                    half, n = divmod(bank, TILES)
                    cols = slice(BANK * half, BANK * (half + 1))
                    banks[j].append(product(
                        lambda a: (w4_w[:, a, P * n : P * (n + 1)].bitcast(FP8X4), w4_sc[ROWS * a : P, P * n : P * (n + 1)]),
                        lambda a: (v_w[a][:, cols].bitcast(FP8X4), packed_v_sc(a, cols)),
                    ))
                else:
                    banks[j].append(feature_bank(bank, lambda a, t: columns(w1_q[a], t), packed_v_sc))

        def to_turns(j):
            if j in TURNS_TAG:
                turns[j] = stage.tile([P, WIDE], F32, name="turns%d" % j, tag=TURNS_TAG[j], align_bytes=64)
            else:
                turns[j] = ring.tile([P, WIDE], F32, name="turns")
            for side, bank in enumerate(banks[j]):
                dst = turns[j][:, BANK * side : BANK * (side + 1)]
                if JOBS[j][0] == "cos":
                    nc.scalar.activation(out=dst, in_=bank, func=ACT.Copy, scale=1.0 / TWO_PI, bias=0.25)
                else:
                    nc.scalar.activation(out=woven(dst), in_=bank, func=ACT.Copy, scale=1.0 / TWO_PI)

        def round_turns(j):
            width = BANK if j == 0 else WIDE
            for lo in range(0, WIDE, width):
                nc.vector.tensor_copy(out=wholes[:, j % DEPTH, lo : lo + width], in_=turns[j][:, lo : lo + width])

        def take_rest(j):
            width = BANK if j == 0 else WIDE
            for lo in range(0, WIDE, width):
                cols = slice(lo, lo + width)
                nc.vector.tensor_tensor(out=rests[:, j % DEPTH, cols], in0=turns[j][:, cols], in1=wholes[:, j % DEPTH, cols], op=SUB)

        def sine(j):
            kind, pair = JOBS[j]
            if kind == "cos":
                dst = cosines[:, WIDE * pair : WIDE * (pair + 1)]
            else:
                sines[j] = ring.tile([P, WIDE], F32, name="sines")
                dst = sines[j][:]
            nc.scalar.activation(out=dst, in_=rests[:, j % DEPTH], func=ACT.Sin, scale=TWO_PI)

        def weigh(j):
            if j in sines:
                scale_by_gain(0, JOBS[j][1], sines[j][:])

        def finish(j):
            if j in sines:
                quantize_h(0, JOBS[j][1])

        stages = (multiply, to_turns, round_turns, take_rest, sine, weigh, finish)
        for step in range(len(JOBS) + len(stages) - 1):
            if step in W1_STEPS:
                w1_q.append(round_w1(len(w1_q)))
            if step == W1_STEPS[-1]:
                tab2_w = stage.tile([P, PASSES, T2], U32, name="tab2_w", tag="big0", align_bytes=64)
                for a in range(PASSES):
                    nc.sync.dma_start(out=tab2_w[:, a, :].bitcast(I32), in_=tab2_words[a].rearrange("p t i -> p (t i)").bitcast(I32))
            for lag, work in enumerate(stages):
                if 0 <= step - lag < len(JOBS):
                    work(step - lag)
            if step == W2_LOAD_STEP:
                w2_raw = stage.tile([P, PASSES, 2 * R], U8, name="w2_raw", tag="w2_raw", align_bytes=64)
                nc.sync.dma_start(out=w2_raw[:].bitcast(I32), in_=w2_words.rearrange("a p n -> p a n").bitcast(I32))
                w2_sc_raw = stage.tile([P, PASSES, R], U8, name="w2_sc_raw", tag="w2_sc_raw", align_bytes=64)
                nc.vector.memset(w2_sc_raw[:].rearrange("p a n -> p (a n)").bitcast(I32), 0)
                for quad in range(QUADS):
                    nc.sync.dma_start(
                        out=w2_sc_raw[32 * quad : 32 * quad + ROWS, :, :].bitcast(I32),
                        in_=w2_scales[:, ROWS * quad : ROWS * (quad + 1), :].rearrange("a r n -> r a n").bitcast(I32),
                    )
            if step == TAB2_SC_STEP:
                tab2_sc = stage.tile([P, T2], U8, name="tab2_sc", tag="tab2_sc", align_bytes=64)
                nc.vector.memset(tab2_sc[:].bitcast(I32), 0)
                load_packed_plane(nc.sync, tab2_sc, tab2_scales)
            if step == W2_DEAL_STEP:
                w2_w = keep.tile([P, PASSES, 2 * R], U8, name="w2_w", align_bytes=64)
                nc.vector.tensor_copy(
                    out=w2_w[:].bitcast(I32).rearrange("p a (t q w) -> p a t q w", t=PACK, w=4),
                    in_=w2_raw[:].bitcast(I32).rearrange("p a (q t w) -> p a t q w", t=PACK, w=4),
                )
                w2_sc = keep.tile([P, PASSES, R], U8, name="w2_sc", align_bytes=64)
                nc.vector.tensor_copy(
                    out=w2_sc[:].bitcast(I32).rearrange("p a (t q w) -> p a t q w", t=PACK, w=2),
                    in_=w2_sc_raw[:].bitcast(I32).rearrange("p a (q t w) -> p a t q w", t=PACK, w=2),
                )
            if step in W3_STEPS:
                w3_q.append(round_on_scalar("w3_%d" % len(w3_q), w3_raw[:, len(w3_q)]))

        v2_sc = stage.tile([P, TRIALS], U8, name="v2_sc", tag="v2_sc", align_bytes=64)
        nc.vector.tensor_copy(out=v2_sc[:], in_=tab2_sc[:].indirect(idx2[:]))
        v2_w = stage.tile([P, PASSES, TRIALS], U32, name="v2_w", tag="wholes", align_bytes=64)
        for a in range(PASSES):
            nc.vector.tensor_copy(out=v2_w[:, a, :], in_=tab2_w[:, a, :].indirect(idx2[:]))

        def w2_columns(a, t):
            return w2_w[:, a, 2 * P * t : 2 * P * (t + 1)].bitcast(FP4X4), w2_sc[:, a, P * t : P * (t + 1)]

        exps = stage.tile([P, DEPTH, WIDE], F32, name="exps", tag="rests", align_bytes=64)
        for step in range(PAIRS + 2):
            if step < PAIRS:
                for side in range(PAIR):
                    bank = feature_bank(PAIR * step + side, w2_columns, lambda a, cols: (v_sc, v_sc_pass1)[a][:, cols])
                    nc.scalar.activation(out=woven(exps[:, step % DEPTH, BANK * side : BANK * (side + 1)]), in_=bank, func=ACT.Exp)
            if 0 <= step - 1 < PAIRS:
                scale_by_gain(1, step - 1, exps[:, (step - 1) % DEPTH])
            if 0 <= step - 2 < PAIRS:
                quantize_h(1, step - 2)
            if step in W5_STEPS:
                w5_q.append(round_on_scalar("w5_%d" % len(w5_q), w5_raw[:, len(w5_q)]))

        scores = [keep.tile([P, S], F32, name="y%d" % n) for n in range(TILES)]

        def second_stage(n, half):
            cols = slice(BANK * half, BANK * (half + 1))
            acc = product(lambda b: columns(w3_q[b], n), lambda b: (h_w[b][:, cols].bitcast(FP8X4), h_sc[b][:, cols]))
            squashed = ring.tile([P, BANK], F32, name="squashed", bufs=DEPTH)
            nc.scalar.activation(out=squashed[:], in_=acc, func=ACT.Tanh)
            bank = TILES * half + n
            nc.vector.tensor_tensor(out=scores[n][:, cols], in0=squashed[:], in1=cosines[:, BANK * bank : BANK * (bank + 1)], op=MULT)

        for n in range(TILES):
            second_stage(n, 0)
        for n in range(TILES):
            second_stage(n, 1)
            acc = product(lambda a: columns(w5_q[a], n), lambda a: (v2_w[:, a, :].bitcast(FP8X4), v2_sc[ROWS * a : P, :]))
            own = ring.tile([P, TRIALS], F32, name="own", bufs=DEPTH)
            nc.scalar.copy(out=own[:], in_=acc)
            result = ring.tile([P, TRIALS], F32, name="result", bufs=DEPTH)
            nc.vector.tensor_tensor(out=result[:], in0=scores[n][:].indirect(picks[:]), in1=own[:], op=ADD)
            nc.sync.dma_start(out=out[P * n : P * (n + 1), :], in_=result[:])
